import numpy as np
import ml_dtypes


def mxq(x, axis, fmt="e4m3"):
    dtype, down = {"e4m3": (ml_dtypes.float8_e4m3fn, 7), "e5m2": (ml_dtypes.float8_e5m2, 14)}[fmt]
    v = np.moveaxis(np.asarray(x, np.float32).astype(ml_dtypes.bfloat16).astype(np.float64), axis, -1)
    blocks = v.reshape(v.shape[:-1] + (-1, 32))
    amax = np.abs(blocks).max(-1, keepdims=True)
    byte = np.maximum(np.where(amax > 0, np.frexp(amax)[1] - 1 + 127, 0) - down, 1)
    scale = np.exp2(byte - 127.0)
    codes = (blocks / scale).astype(np.float32).astype(dtype).astype(np.float64)
    return np.moveaxis((codes * scale).reshape(v.shape), -1, axis)


WIDE = False


def mx_kscale(k):
    if not WIDE:
        return np.ones(k)
    levels = np.array([10, -10, 5, -5, 0])
    if k % 512:
        return np.exp2(np.random.permutation(np.resize(levels, k // 32))).repeat(32)
    a = np.empty((k // 512, 16))
    for p in range(k // 512):
        a[p, :8] = np.random.permutation(np.resize(levels, 8))
        for g in range(8):
            far = levels[np.abs(levels - a[p, g]) >= 10]
            a[p, g + 8] = far[np.random.randint(len(far))]
    return np.exp2(a.ravel()).repeat(32)


def f64(x):
    return np.asarray(x).astype(np.float64)


def striped(idx):
    return np.tile(idx.reshape(-1, 16).T, (8, 1)).astype(np.uint16)


def unstriped(offs):
    return offs[:16].T.reshape(-1).astype(np.int64)


E2M1 = np.array([0.0, 0.5, 1.0, 1.5, 2.0, 3.0, 4.0, 6.0, -0.0, -0.5, -1.0, -1.5, -2.0, -3.0, -4.0, -6.0])


def pack_weight(w, fmt):
    k, n = w.shape
    w = f64(np.asarray(w, np.float32).astype(ml_dtypes.bfloat16)).reshape(k // 32, 32, n)
    amax = np.abs(w).max(1)
    if fmt == "e4m3":
        byte = np.frexp(amax)[1] - 1 + 127 - 7
    else:
        mant, ex = np.frexp(amax / 6.0)
        byte = np.where(mant > 0.5, ex, ex - 1) + 127
    byte = np.clip(np.where(amax > 0, byte, 1), 1, 254)
    scaled = (w * np.exp2(127.0 - byte)[:, None, :]).reshape(k, n).astype(np.float32)
    by_word = np.ascontiguousarray(scaled.reshape(k // 512, 128, 4, n).transpose(0, 1, 3, 2))
    if fmt == "e4m3":
        words = by_word.astype(ml_dtypes.float8_e4m3fn).view(np.uint8)
    else:
        c = by_word.astype(ml_dtypes.float4_e2m1fn).view(np.uint8) & 0xF
        words = (c[..., 0::2] | (c[..., 1::2] << 4)).reshape(k // 512, 128, 2 * n)
    return np.ascontiguousarray(words), np.ascontiguousarray(byte.astype(np.uint8).reshape(k // 512, 16, n))


def unpack_weight(words, scales, fmt):
    g, _, n = scales.shape
    words = np.ascontiguousarray(words).reshape(g, 128, n, -1)
    if fmt == "e4m3":
        vals = words.view(ml_dtypes.float8_e4m3fn).astype(np.float64)
    else:
        nib = np.empty((g, 128, n, 4), np.uint8)
        nib[..., 0::2] = words & 0xF
        nib[..., 1::2] = words >> 4
        vals = E2M1[nib]
    vals = vals * np.repeat(np.exp2(scales.astype(np.float64) - 127.0), 8, axis=1)[..., None]
    return vals.transpose(0, 1, 3, 2).reshape(g * 512, n)


def silu(v):
    return v / (1.0 + np.exp(-np.maximum(v, -700.0)))


K, T, E, C, H, N = 512, 512, 12, 128, 512, 256


def by_expert(wq, xq):
    return np.concatenate([wq[e].T @ xq[:, e * C:(e + 1) * C] for e in range(E)], axis=1)


def setup_inputs():
    n = np.random.standard_normal
    s = mx_kscale(K)
    u = mx_kscale(H)
    slot_token = np.concatenate([np.random.permutation(T)[:C] for e in range(E)])
    partner = np.concatenate([np.random.permutation(T) for _ in range(-(-E * C // T))])[:E * C]
    x = pack_weight(n((K, T)) * s[:, None], "e4m3")
    w1 = [pack_weight(m, "e2m1") for m in n((E, K, H)) / np.sqrt(K) / s[None, :, None] * u]
    wp = [pack_weight(m, "e4m3") for m in n((E, K, H)) / np.sqrt(K) / s[None, :, None] * u]
    w2 = [pack_weight(m, "e2m1") for m in n((E, H, N)) / np.sqrt(H) / u[None, :, None]]
    return {
        "x_words": x[0],
        "x_scales": x[1],
        "w1_words": np.stack([m[0] for m in w1]),
        "w1_scales": np.stack([m[1] for m in w1]),
        "wp_words": np.stack([m[0] for m in wp]),
        "wp_scales": np.stack([m[1] for m in wp]),
        "w2_words": np.stack([m[0] for m in w2]),
        "w2_scales": np.stack([m[1] for m in w2]),
        "offs": striped(slot_token),
        "offs2": striped(partner),
    }


def reference(x_words, x_scales, w1_words, w1_scales, wp_words, wp_scales, w2_words, w2_scales, offs, offs2):
    w1 = np.stack([unpack_weight(w1_words[e], w1_scales[e], "e2m1") for e in range(E)])
    wp = np.stack([unpack_weight(wp_words[e], wp_scales[e], "e4m3") for e in range(E)])
    w2 = np.stack([unpack_weight(w2_words[e], w2_scales[e], "e2m1") for e in range(E)])
    idx, idx2 = unstriped(offs), unstriped(offs2)
    x = unpack_weight(x_words, x_scales, "e4m3")
    h = silu(by_expert(w1, x[:, idx]) + by_expert(wp, x[:, idx2]))
    y = by_expert(w2, mxq(h, 0, "e4m3"))
    out = y
    return out

@@ -1,0 +1,192 @@
+from contextlib import ExitStack
+
+import concourse.mybir as mybir
+from concourse.masks import make_identity
+
+K, T, E, C, H, N = 512, 512, 12, 128, 512, 256
+FLOPS = 2 * E * C * (2 * K * H + H * N)
+
+F32 = mybir.dt.float32
+BF16 = mybir.dt.bfloat16
+I32 = mybir.dt.int32
+U32 = mybir.dt.uint32
+U16 = mybir.dt.uint16
+U8 = mybir.dt.uint8
+FP8X4 = mybir.dt.float8_e4m3fn_x4
+FP4X4 = mybir.dt.float4_e2m1fn_x4
+SILU = mybir.ActivationFunctionType.Silu
+
+P = 128
+GROUPS = [(0, 2), (2, 4), (4, 6), (6, 8), (8, 10), (10, 11), (11, 12)]
+W_CHUNKS = [(0, 2), (2, 4), (4, 6), (6, 8), (8, 10), (10, 12)]
+LAG = 3
+REGION = 2560
+BANK = 2048
+TURN_BANK = [4, 5, 4, 5, 4, 5, 4]
+Y_BANK = [2, 0, 2, 3, 6, 7, 1]
+
+
+def tile_moe_duo_s_silu_kernel(
+    tc, x_words, x_scales, w1_words, w1_scales, wp_words, wp_scales, w2_words, w2_scales, offs, offs2, out
+):
+    nc = tc.nc
+    with ExitStack() as ctx:
+        keep = ctx.enter_context(tc.tile_pool(name="keep", bufs=1))
+        shared = ctx.enter_context(tc.tile_pool(name="shared", bufs=1))
+        psum = ctx.enter_context(tc.psum_pool(name="psum", bufs=1))
+
+        own_list = keep.tile([P, E * C // 16], U16, name="own_list")
+        partner_list = keep.tile([P, E * C // 16], U16, name="partner_list")
+        xw = keep.tile([P, T], I32, name="xw", align_bytes=64)
+        xs = keep.tile([P, T], U8, name="xs", align_bytes=64)
+        s1p = keep.tile([P, E - 1, H], U8, name="s1p", align_bytes=64)
+        s1p_last = keep.tile([P, H], U8, name="s1p_last", align_bytes=64)
+        s2 = keep.tile([P, E, N], U8, name="s2", align_bytes=64)
+        ident = keep.tile([P, P], F32, name="ident", align_bytes=64)
+        warm_in = keep.tile([P, 1], F32, name="warm_in")
+        warm_out = keep.tile([P, 1], F32, name="warm_out")
+
+        nc.gpsimd.memset(warm_in[:], 0.0)
+
+        w1_src = w1_words.rearrange("e s p b -> p (e s) b").bitcast(I32)
+        wp_src = wp_words.rearrange("e s p i d -> p (e s) (i d)").bitcast(I32)
+        w2_src = w2_words.rearrange("e s p b -> p (e s) b").bitcast(I32)
+        xs_rows = x_scales.rearrange("s (q r) t -> r q s t", r=4).bitcast(I32)
+        s1_rows = w1_scales.rearrange("e s b n -> (e s b) n").bitcast(I32)
+        sp_rows = wp_scales.rearrange("e s b n -> (e s b) n").bitcast(I32)
+        s2_rows = w2_scales.rearrange("e s (q r) n -> r q (e s) n", r=4).bitcast(I32)
+        s1p_i = s1p[:].bitcast(I32)
+        s2_i = s2[:].bitcast(I32)
+        xs_i = xs[:].bitcast(I32)
+
+        w1, wp, w2 = {}, {}, {}
+
+        def load_weights(store, name, src, width, lo, hi, queue):
+            t = keep.tile([P, hi - lo, width], U8, name="%s_%d" % (name, lo), align_bytes=64)
+            queue.dma_start(out=t[:].bitcast(I32), in_=src[:, lo:hi, :])
+            for e in range(lo, hi):
+                store[e] = t[:, e - lo, :]
+
+        def load_plane_rows(rows, first, r, queue):
+            experts = E - 1
+            queue.dma_start(
+                out=s1p_i[first + r : P : 8, 0:experts, :],
+                in_=rows[r : r + 16 * experts, :].rearrange("(e m) n -> m e n", m=16),
+            )
+
+        def load_last_rows(rows, first, r, queue):
+            queue.dma_start(out=s1p_last[:].bitcast(I32)[first + r : P : 32, :], in_=rows[16 * (E - 1) + r : 16 * E : 4, :])
+
+        for r in range(4):
+            queue = nc.scalar if r < 2 else nc.sync
+            queue.dma_start(out=xs_i[r:P:4, :], in_=xs_rows[r].to_broadcast([4, 8, T // 4]))
+        nc.scalar.dma_start(out=xw[:], in_=x_words.rearrange("s p t d -> p (s t d)").bitcast(I32))
+        nc.sync.dma_start(own_list[:], offs)
+        nc.sync.dma_start(partner_list[:], offs2)
+        nc.scalar.activation(warm_out[:], warm_in[:], SILU)
+
+        load_weights(w1, "w1", w1_src, 2 * H, 0, 2, nc.gpsimd)
+        make_identity(nc, ident[:])
+        nc.gpsimd.memset(s2_i, 0)
+        nc.gpsimd.memset(s1p_last[:].bitcast(I32), 0)
+        for r in range(4):
+            nc.gpsimd.dma_start(out=s2_i[r:P:32, :, :], in_=s2_rows[r])
+        for r in range(4):
+            load_last_rows(s1_rows, 0, r, nc.gpsimd)
+            load_last_rows(sp_rows, 4, r, nc.gpsimd)
+        for j, (lo, hi) in enumerate(W_CHUNKS):
+            load_weights(wp, "wp", wp_src, 4 * H, lo, hi, nc.sync)
+            if j == 0:
+                for r in range(4):
+                    load_plane_rows(s1_rows, 0, r, nc.sync)
+                    load_plane_rows(sp_rows, 4, r, nc.sync if r == 0 else nc.scalar)
+            else:
+                load_weights(w1, "w1", w1_src, 2 * H, lo, hi, nc.sync)
+            if j == 3:
+                load_weights(w2, "w2", w2_src, 2 * N, 0, E, nc.sync)
+
+        x_window = xw[:].bitcast(U32)
+        out_view = out.rearrange("(h p) s -> p h s", p=P)
+        grouped = {}
+        activated = {}
+
+        def first_layer(i):
+            lo, hi = GROUPS[i]
+            n = (hi - lo) * C
+            cols = slice(lo * C // 16, hi * C // 16)
+            gathered = []
+            base = i * REGION
+            for name, lst, at_words, at_scales in (("own", own_list, 0, 1024), ("partner", partner_list, 1536, 1280)):
+                words = shared.tile([P, n], U32, name="%s_words_%d" % (name, lo), align_bytes=64, offset=base + at_words)
+                scales = shared.tile([P, n], U8, name="%s_scales_%d" % (name, lo), align_bytes=64, offset=base + at_scales)
+                nc.vector.tensor_copy(words[:], x_window.indirect(lst[:, cols]))
+                nc.vector.tensor_copy(scales[:], xs[:].indirect(lst[:, cols]))
+                gathered.append((words, scales))
+            hs = []
+            for e in range(lo, hi):
+                sl = slice((e - lo) * C, (e - lo + 1) * C)
+                pre = psum.tile([P, H], F32, name="pre_%d" % e, offset=(e % 4) * BANK)
+                plane = s1p[:, e, :] if e < E - 1 else s1p_last[:]
+                nc.tensor.matmul_mx(
+                    out=pre[:], lhsT=gathered[0][0][:, sl].bitcast(FP8X4), lhsT_scale=gathered[0][1][:, sl],
+                    rhs=w1[e].bitcast(FP4X4), rhs_scale=plane, start=True, stop=False,
+                )
+                nc.tensor.matmul_mx(
+                    out=pre[:], lhsT=gathered[1][0][:, sl].bitcast(FP8X4), lhsT_scale=gathered[1][1][:, sl],
+                    rhs=wp[e].bitcast(FP8X4), rhs_scale=plane[4:P, :], start=False, stop=True,
+                )
+                h = keep.tile([P, H], BF16, name="h_%d" % e, align_bytes=64)
+                nc.scalar.activation(
+                    h[:].rearrange("s (u p d) -> s u p d", u=2, d=2),
+                    pre[:].rearrange("s (p u d) -> s u p d", u=2, d=2),
+                    SILU,
+                )
+                hs.append(h)
+            activated[i] = hs
+
+        def turn(i):
+            lo, hi = GROUPS[i]
+            n = (hi - lo) * C
+            bank = TURN_BANK[i]
+            turned = psum.tile([P, hi - lo, 2, C], F32, name="turned_%d" % lo, offset=bank * BANK)
+            for j, h in enumerate(activated[i]):
+                pairs = h[:].bitcast(F32)
+                for u in range(2):
+                    nc.tensor.transpose(turned[:, j, u, :], pairs[:, u * P : (u + 1) * P], ident[:])
+            ht = shared.tile([P, 4 * n], BF16, name="ht_%d" % lo, align_bytes=64, offset=(i + LAG + 1) * REGION + 256)
+            nc.scalar.copy(
+                ht[:].bitcast(F32).rearrange("p (e s u) -> p e s u", u=2, s=C),
+                turned[:].rearrange("p e u s -> p e s u"),
+            )
+            grouped[lo] = ht
+
+        def second_layer(i):
+            lo, hi = GROUPS[i]
+            n = (hi - lo) * C
+            codes = keep.tile([P, n], U32, name="h_codes_%d" % lo, align_bytes=64)
+            scales = keep.tile([P, n], U8, name="h_scales_%d" % lo, align_bytes=64)
+            nc.vector.quantize_mx(out=codes[:].bitcast(FP8X4), scales=scales[:], in_=grouped[lo][:])
+            y = psum.tile([P, 2, n], F32, name="y_%d" % lo, offset=Y_BANK[i] * BANK)
+            for e in range(lo, hi):
+                sl = slice((e - lo) * C, (e - lo + 1) * C)
+                for half in range(2):
+                    nc.tensor.matmul_mx(
+                        out=y[:, half, sl],
+                        lhsT=w2[e][:, half * 2 * P : (half + 1) * 2 * P].bitcast(FP4X4),
+                        lhsT_scale=s2[:, e, half * P : (half + 1) * P],
+                        rhs=codes[:, sl].bitcast(FP8X4), rhs_scale=scales[:, sl], start=True, stop=True,
+                    )
+            staged = keep.tile([P, 2, n], F32, name="staged_%d" % lo)
+            if i >= 3:
+                nc.vector.tensor_copy(staged[:], y[:])
+            else:
+                nc.scalar.copy(staged[:], y[:])
+            nc.sync.dma_start(out=out_view[:, :, lo * C : hi * C], in_=staged[:])
+
+        for i in range(len(GROUPS) + LAG):
+            if i < len(GROUPS):
+                first_layer(i)
+            if 1 <= i <= len(GROUPS):
+                turn(i - 1)
+            if i >= LAG:
+                second_layer(i - LAG)

@@ -17,13 +17,16 @@ FP4X4 = mybir.dt.float4_e2m1fn_x4
 SILU = mybir.ActivationFunctionType.Silu
 
 P = 128
+PAIRS = E // 2
 GROUPS = [(0, 2), (2, 4), (4, 6), (6, 8), (8, 10), (10, 11), (11, 12)]
-W_CHUNKS = [(0, 2), (2, 4), (4, 6), (6, 8), (8, 10), (10, 12)]
+W2_AFTER = {3: (0, 2), 4: (2, 4), 5: (4, 12)}
 LAG = 3
 REGION = 2560
 BANK = 2048
-TURN_BANK = [4, 5, 4, 5, 4, 5, 4]
-Y_BANK = [2, 0, 2, 3, 6, 7, 1]
+TURN_BANK = [2, 0, 2, 0, 2, 4, 5]
+Y_BANK = [6, 7, 6, 7, 1, 3, 0]
+Y_ON_VECTOR = (2, 4, 6)
+TURN_ON_VECTOR = (4,)
 
 
 def tile_moe_duo_s_silu_kernel(
@@ -39,26 +42,22 @@ def tile_moe_duo_s_silu_kernel(
         partner_list = keep.tile([P, E * C // 16], U16, name="partner_list")
         xw = keep.tile([P, T], I32, name="xw", align_bytes=64)
         xs = keep.tile([P, T], U8, name="xs", align_bytes=64)
-        s1p = keep.tile([P, E - 1, H], U8, name="s1p", align_bytes=64)
-        s1p_last = keep.tile([P, H], U8, name="s1p_last", align_bytes=64)
+        s1 = keep.tile([P, E, H], U8, name="s1", align_bytes=64)
+        sp = keep.tile([P, E, H], U8, name="sp", align_bytes=64)
         s2 = keep.tile([P, E, N], U8, name="s2", align_bytes=64)
         ident = keep.tile([P, P], F32, name="ident", align_bytes=64)
         warm_in = keep.tile([P, 1], F32, name="warm_in")
         warm_out = keep.tile([P, 1], F32, name="warm_out")
 
         nc.gpsimd.memset(warm_in[:], 0.0)
+        nc.vector.memset(s1[:].bitcast(I32), 0)
+        nc.gpsimd.memset(sp[:].bitcast(I32), 0)
+        nc.gpsimd.memset(s2[:].bitcast(I32), 0)
+        make_identity(nc, ident[:])
 
         w1_src = w1_words.rearrange("e s p b -> p (e s) b").bitcast(I32)
         wp_src = wp_words.rearrange("e s p i d -> p (e s) (i d)").bitcast(I32)
         w2_src = w2_words.rearrange("e s p b -> p (e s) b").bitcast(I32)
-        xs_rows = x_scales.rearrange("s (q r) t -> r q s t", r=4).bitcast(I32)
-        s1_rows = w1_scales.rearrange("e s b n -> (e s b) n").bitcast(I32)
-        sp_rows = wp_scales.rearrange("e s b n -> (e s b) n").bitcast(I32)
-        s2_rows = w2_scales.rearrange("e s (q r) n -> r q (e s) n", r=4).bitcast(I32)
-        s1p_i = s1p[:].bitcast(I32)
-        s2_i = s2[:].bitcast(I32)
-        xs_i = xs[:].bitcast(I32)
-
         w1, wp, w2 = {}, {}, {}
 
         def load_weights(store, name, src, width, lo, hi, queue):
@@ -67,73 +66,63 @@ def tile_moe_duo_s_silu_kernel(
             for e in range(lo, hi):
                 store[e] = t[:, e - lo, :]
 
-        def load_plane_rows(rows, first, r, queue):
-            experts = E - 1
-            queue.dma_start(
-                out=s1p_i[first + r : P : 8, 0:experts, :],
-                in_=rows[r : r + 16 * experts, :].rearrange("(e m) n -> m e n", m=16),
-            )
+        def load_scale_rows(plane, rows, first, r, queue):
+            queue.dma_start(out=plane.bitcast(I32)[first + r : P : 32], in_=rows.bitcast(I32)[r])
 
-        def load_last_rows(rows, first, r, queue):
-            queue.dma_start(out=s1p_last[:].bitcast(I32)[first + r : P : 32, :], in_=rows[16 * (E - 1) + r : 16 * E : 4, :])
+        xs_rows = x_scales.rearrange("s (q r) t -> r q s t", r=4).bitcast(I32)
+        s1_rows = w1_scales.rearrange("e s (q r) n -> r q (e s) n", r=4)
+        sp_rows = wp_scales.rearrange("e s (q r) n -> r q (e s) n", r=4)
+        s2_rows = w2_scales.rearrange("e s (q r) n -> r q (e s) n", r=4)
 
         for r in range(4):
             queue = nc.scalar if r < 2 else nc.sync
-            queue.dma_start(out=xs_i[r:P:4, :], in_=xs_rows[r].to_broadcast([4, 8, T // 4]))
+            queue.dma_start(out=xs[:].bitcast(I32)[r:P:4, :], in_=xs_rows[r].to_broadcast([4, 8, T // 4]))
         nc.scalar.dma_start(out=xw[:], in_=x_words.rearrange("s p t d -> p (s t d)").bitcast(I32))
         nc.sync.dma_start(own_list[:], offs)
         nc.sync.dma_start(partner_list[:], offs2)
         nc.scalar.activation(warm_out[:], warm_in[:], SILU)
 
-        load_weights(w1, "w1", w1_src, 2 * H, 0, 2, nc.gpsimd)
-        make_identity(nc, ident[:])
-        nc.gpsimd.memset(s2_i, 0)
-        nc.gpsimd.memset(s1p_last[:].bitcast(I32), 0)
-        for r in range(4):
-            nc.gpsimd.dma_start(out=s2_i[r:P:32, :, :], in_=s2_rows[r])
-        for r in range(4):
-            load_last_rows(s1_rows, 0, r, nc.gpsimd)
-            load_last_rows(sp_rows, 4, r, nc.gpsimd)
-        for j, (lo, hi) in enumerate(W_CHUNKS):
-            load_weights(wp, "wp", wp_src, 4 * H, lo, hi, nc.sync)
+        for j in range(PAIRS):
+            load_weights(wp, "wp", wp_src, 4 * H, 2 * j, 2 * j + 2, nc.sync)
+            load_weights(w1, "w1", w1_src, 2 * H, 2 * j, 2 * j + 2, nc.sync)
             if j == 0:
                 for r in range(4):
-                    load_plane_rows(s1_rows, 0, r, nc.sync)
-                    load_plane_rows(sp_rows, 4, r, nc.sync if r == 0 else nc.scalar)
-            else:
-                load_weights(w1, "w1", w1_src, 2 * H, lo, hi, nc.sync)
-            if j == 3:
-                load_weights(w2, "w2", w2_src, 2 * N, 0, E, nc.sync)
+                    load_scale_rows(s1[:], s1_rows, 0, r, nc.sync)
+                for r in range(4):
+                    load_scale_rows(sp[:], sp_rows, 4, r, nc.sync)
+            if j == 2:
+                for r in range(4):
+                    load_scale_rows(s2[:], s2_rows, 0, r, nc.sync)
+            if j in W2_AFTER:
+                load_weights(w2, "w2", w2_src, 2 * N, W2_AFTER[j][0], W2_AFTER[j][1], nc.sync)
 
         x_window = xw[:].bitcast(U32)
         out_view = out.rearrange("(h p) s -> p h s", p=P)
         grouped = {}
         activated = {}
 
-        def first_layer(i):
-            lo, hi = GROUPS[i]
-            n = (hi - lo) * C
-            cols = slice(lo * C // 16, hi * C // 16)
+        def first_layer(j):
             gathered = []
-            base = i * REGION
+            base = j * REGION
             for name, lst, at_words, at_scales in (("own", own_list, 0, 1024), ("partner", partner_list, 1536, 1280)):
-                words = shared.tile([P, n], U32, name="%s_words_%d" % (name, lo), align_bytes=64, offset=base + at_words)
-                scales = shared.tile([P, n], U8, name="%s_scales_%d" % (name, lo), align_bytes=64, offset=base + at_scales)
-                nc.vector.tensor_copy(words[:], x_window.indirect(lst[:, cols]))
-                nc.vector.tensor_copy(scales[:], xs[:].indirect(lst[:, cols]))
+                words = shared.tile([P, 2 * C], U32, name="%s_words_%d" % (name, j), align_bytes=64, offset=base + at_words)
+                scales = shared.tile([P, 2 * C], U8, name="%s_scales_%d" % (name, j), align_bytes=64, offset=base + at_scales)
+                step = C if (j == PAIRS - 1 and name == "partner") else 2 * C
+                for c0 in range(0, 2 * C, step):
+                    cols = slice((2 * j * C + c0) // 16, (2 * j * C + c0 + step) // 16)
+                    nc.vector.tensor_copy(words[:, c0 : c0 + step], x_window.indirect(lst[:, cols]))
+                    nc.vector.tensor_copy(scales[:, c0 : c0 + step], xs[:].indirect(lst[:, cols]))
                 gathered.append((words, scales))
-            hs = []
-            for e in range(lo, hi):
-                sl = slice((e - lo) * C, (e - lo + 1) * C)
+            for e in (2 * j, 2 * j + 1):
+                sl = slice((e % 2) * C, (e % 2 + 1) * C)
                 pre = psum.tile([P, H], F32, name="pre_%d" % e, offset=(e % 4) * BANK)
-                plane = s1p[:, e, :] if e < E - 1 else s1p_last[:]
                 nc.tensor.matmul_mx(
                     out=pre[:], lhsT=gathered[0][0][:, sl].bitcast(FP8X4), lhsT_scale=gathered[0][1][:, sl],
-                    rhs=w1[e].bitcast(FP4X4), rhs_scale=plane, start=True, stop=False,
+                    rhs=w1[e].bitcast(FP4X4), rhs_scale=s1[:, e, :], start=True, stop=False,
                 )
                 nc.tensor.matmul_mx(
                     out=pre[:], lhsT=gathered[1][0][:, sl].bitcast(FP8X4), lhsT_scale=gathered[1][1][:, sl],
-                    rhs=wp[e].bitcast(FP8X4), rhs_scale=plane[4:P, :], start=False, stop=True,
+                    rhs=wp[e].bitcast(FP8X4), rhs_scale=sp[4:P, e, :], start=False, stop=True,
                 )
                 h = keep.tile([P, H], BF16, name="h_%d" % e, align_bytes=64)
                 nc.scalar.activation(
@@ -141,20 +130,19 @@ def tile_moe_duo_s_silu_kernel(
                     pre[:].rearrange("s (p u d) -> s u p d", u=2, d=2),
                     SILU,
                 )
-                hs.append(h)
-            activated[i] = hs
+                activated[e] = h
 
         def turn(i):
             lo, hi = GROUPS[i]
             n = (hi - lo) * C
-            bank = TURN_BANK[i]
-            turned = psum.tile([P, hi - lo, 2, C], F32, name="turned_%d" % lo, offset=bank * BANK)
-            for j, h in enumerate(activated[i]):
-                pairs = h[:].bitcast(F32)
+            turned = psum.tile([P, hi - lo, 2, C], F32, name="turned_%d" % lo, offset=TURN_BANK[i] * BANK)
+            for e in range(lo, hi):
+                pairs = activated[e][:].bitcast(F32)
                 for u in range(2):
-                    nc.tensor.transpose(turned[:, j, u, :], pairs[:, u * P : (u + 1) * P], ident[:])
+                    nc.tensor.transpose(turned[:, e - lo, u, :], pairs[:, u * P : (u + 1) * P], ident[:])
             ht = shared.tile([P, 4 * n], BF16, name="ht_%d" % lo, align_bytes=64, offset=(i + LAG + 1) * REGION + 256)
-            nc.scalar.copy(
+            copy = nc.vector.tensor_copy if i in TURN_ON_VECTOR else nc.scalar.copy
+            copy(
                 ht[:].bitcast(F32).rearrange("p (e s u) -> p e s u", u=2, s=C),
                 turned[:].rearrange("p e u s -> p e s u"),
             )
@@ -177,14 +165,14 @@ def tile_moe_duo_s_silu_kernel(
                         rhs=codes[:, sl].bitcast(FP8X4), rhs_scale=scales[:, sl], start=True, stop=True,
                     )
             staged = keep.tile([P, 2, n], F32, name="staged_%d" % lo)
-            if i >= 3:
+            if i in Y_ON_VECTOR:
                 nc.vector.tensor_copy(staged[:], y[:])
             else:
                 nc.scalar.copy(staged[:], y[:])
             nc.sync.dma_start(out=out_view[:, :, lo * C : hi * C], in_=staged[:])
 
         for i in range(len(GROUPS) + LAG):
-            if i < len(GROUPS):
+            if i < PAIRS:
                 first_layer(i)
             if 1 <= i <= len(GROUPS):
                 turn(i - 1)

@@ -20,6 +20,7 @@ P = 128
 PAIRS = E // 2
 GROUPS = [(0, 2), (2, 4), (4, 6), (6, 8), (8, 10), (10, 11), (11, 12)]
 W2_AFTER = {3: (0, 2), 4: (2, 4), 5: (4, 12)}
+STORE_FROM = {4: 0, 8: 4, 10: 8, 11: 10, 12: 11}
 LAG = 3
 REGION = 2560
 BANK = 2048
@@ -42,17 +43,15 @@ def tile_moe_duo_s_silu_kernel(
         partner_list = keep.tile([P, E * C // 16], U16, name="partner_list")
         xw = keep.tile([P, T], I32, name="xw", align_bytes=64)
         xs = keep.tile([P, T], U8, name="xs", align_bytes=64)
-        s1 = keep.tile([P, E, H], U8, name="s1", align_bytes=64)
-        sp = keep.tile([P, E, H], U8, name="sp", align_bytes=64)
+        s1p = keep.tile([P, E, H], U8, name="s1p", align_bytes=64)
         s2 = keep.tile([P, E, N], U8, name="s2", align_bytes=64)
         ident = keep.tile([P, P], F32, name="ident", align_bytes=64)
         warm_in = keep.tile([P, 1], F32, name="warm_in")
         warm_out = keep.tile([P, 1], F32, name="warm_out")
 
+        nc.gpsimd.memset(xs[:].bitcast(I32), 0)
         nc.gpsimd.memset(warm_in[:], 0.0)
-        nc.vector.memset(s1[:].bitcast(I32), 0)
-        nc.gpsimd.memset(sp[:].bitcast(I32), 0)
-        nc.gpsimd.memset(s2[:].bitcast(I32), 0)
+        nc.vector.memset(s1p[:].bitcast(I32), 0)
         make_identity(nc, ident[:])
 
         w1_src = w1_words.rearrange("e s p b -> p (e s) b").bitcast(I32)
@@ -69,35 +68,36 @@ def tile_moe_duo_s_silu_kernel(
         def load_scale_rows(plane, rows, first, r, queue):
             queue.dma_start(out=plane.bitcast(I32)[first + r : P : 32], in_=rows.bitcast(I32)[r])
 
-        xs_rows = x_scales.rearrange("s (q r) t -> r q s t", r=4).bitcast(I32)
+        xs_rows = x_scales.rearrange("s (q r) t -> r q (s t)", r=4)
         s1_rows = w1_scales.rearrange("e s (q r) n -> r q (e s) n", r=4)
         sp_rows = wp_scales.rearrange("e s (q r) n -> r q (e s) n", r=4)
         s2_rows = w2_scales.rearrange("e s (q r) n -> r q (e s) n", r=4)
 
-        for r in range(4):
-            queue = nc.scalar if r < 2 else nc.sync
-            queue.dma_start(out=xs[:].bitcast(I32)[r:P:4, :], in_=xs_rows[r].to_broadcast([4, 8, T // 4]))
-        nc.scalar.dma_start(out=xw[:], in_=x_words.rearrange("s p t d -> p (s t d)").bitcast(I32))
         nc.sync.dma_start(own_list[:], offs)
+        for r in range(4):
+            load_scale_rows(xs[:], xs_rows, 0, r, nc.scalar if r < 2 else nc.sync)
         nc.sync.dma_start(partner_list[:], offs2)
+        nc.sync.dma_start(out=xw[:], in_=x_words.rearrange("s p t d -> p (s t d)").bitcast(I32))
         nc.scalar.activation(warm_out[:], warm_in[:], SILU)
+
+        for r in range(4):
+            load_scale_rows(s1p[:], sp_rows, 4, r, nc.gpsimd)
+        nc.gpsimd.memset(s2[:].bitcast(I32), 0)
+        for r in range(4):
+            load_scale_rows(s2[:], s2_rows, 0, r, nc.gpsimd)
 
         for j in range(PAIRS):
             load_weights(wp, "wp", wp_src, 4 * H, 2 * j, 2 * j + 2, nc.sync)
             load_weights(w1, "w1", w1_src, 2 * H, 2 * j, 2 * j + 2, nc.sync)
             if j == 0:
                 for r in range(4):
-                    load_scale_rows(s1[:], s1_rows, 0, r, nc.sync)
-                for r in range(4):
-                    load_scale_rows(sp[:], sp_rows, 4, r, nc.sync)
-            if j == 2:
-                for r in range(4):
-                    load_scale_rows(s2[:], s2_rows, 0, r, nc.sync)
+                    load_scale_rows(s1p[:], s1_rows, 0, r, nc.sync)
             if j in W2_AFTER:
                 load_weights(w2, "w2", w2_src, 2 * N, W2_AFTER[j][0], W2_AFTER[j][1], nc.sync)
 
         x_window = xw[:].bitcast(U32)
         out_view = out.rearrange("(h p) s -> p h s", p=P)
+        staged = keep.tile([P, 2, E * C], F32, name="staged")
         grouped = {}
         activated = {}
 
@@ -118,11 +118,11 @@ def tile_moe_duo_s_silu_kernel(
                 pre = psum.tile([P, H], F32, name="pre_%d" % e, offset=(e % 4) * BANK)
                 nc.tensor.matmul_mx(
                     out=pre[:], lhsT=gathered[0][0][:, sl].bitcast(FP8X4), lhsT_scale=gathered[0][1][:, sl],
-                    rhs=w1[e].bitcast(FP4X4), rhs_scale=s1[:, e, :], start=True, stop=False,
+                    rhs=w1[e].bitcast(FP4X4), rhs_scale=s1p[:, e, :], start=True, stop=False,
                 )
                 nc.tensor.matmul_mx(
                     out=pre[:], lhsT=gathered[1][0][:, sl].bitcast(FP8X4), lhsT_scale=gathered[1][1][:, sl],
-                    rhs=wp[e].bitcast(FP8X4), rhs_scale=sp[4:P, e, :], start=False, stop=True,
+                    rhs=wp[e].bitcast(FP8X4), rhs_scale=s1p[4:P, e, :], start=False, stop=True,
                 )
                 h = keep.tile([P, H], BF16, name="h_%d" % e, align_bytes=64)
                 nc.scalar.activation(
@@ -164,12 +164,11 @@ def tile_moe_duo_s_silu_kernel(
                         lhsT_scale=s2[:, e, half * P : (half + 1) * P],
                         rhs=codes[:, sl].bitcast(FP8X4), rhs_scale=scales[:, sl], start=True, stop=True,
                     )
-            staged = keep.tile([P, 2, n], F32, name="staged_%d" % lo)
-            if i in Y_ON_VECTOR:
-                nc.vector.tensor_copy(staged[:], y[:])
-            else:
-                nc.scalar.copy(staged[:], y[:])
-            nc.sync.dma_start(out=out_view[:, :, lo * C : hi * C], in_=staged[:])
+            copy = nc.vector.tensor_copy if i in Y_ON_VECTOR else nc.scalar.copy
+            copy(staged[:, :, lo * C : hi * C], y[:])
+            if hi in STORE_FROM:
+                cols = slice(STORE_FROM[hi] * C, hi * C)
+                nc.sync.dma_start(out=out_view[:, :, cols], in_=staged[:, :, cols])
 
         for i in range(len(GROUPS) + LAG):
             if i < PAIRS:

@@ -21,6 +21,7 @@ PAIRS = E // 2
 GROUPS = [(0, 2), (2, 4), (4, 6), (6, 8), (8, 10), (10, 11), (11, 12)]
 W2_AFTER = {3: (0, 2), 4: (2, 4), 5: (4, 12)}
 STORE_FROM = {4: 0, 8: 4, 10: 8, 11: 10, 12: 11}
+SMALL_AFTER = [0, 0, 3, 6, 9, 12, 12]
 LAG = 3
 REGION = 2560
 BANK = 2048
@@ -43,7 +44,8 @@ def tile_moe_duo_s_silu_kernel(
         partner_list = keep.tile([P, E * C // 16], U16, name="partner_list")
         xw = keep.tile([P, T], I32, name="xw", align_bytes=64)
         xs = keep.tile([P, T], U8, name="xs", align_bytes=64)
-        s1p = keep.tile([P, E, H], U8, name="s1p", align_bytes=64)
+        s1p = keep.tile([P, E - 1, H], U8, name="s1p", align_bytes=64)
+        s1p_last = keep.tile([P, H], U8, name="s1p_last", align_bytes=64)
         s2 = keep.tile([P, E, N], U8, name="s2", align_bytes=64)
         ident = keep.tile([P, P], F32, name="ident", align_bytes=64)
         warm_in = keep.tile([P, 1], F32, name="warm_in")
@@ -51,8 +53,6 @@ def tile_moe_duo_s_silu_kernel(
 
         nc.gpsimd.memset(xs[:].bitcast(I32), 0)
         nc.gpsimd.memset(warm_in[:], 0.0)
-        nc.vector.memset(s1p[:].bitcast(I32), 0)
-        make_identity(nc, ident[:])
 
         w1_src = w1_words.rearrange("e s p b -> p (e s) b").bitcast(I32)
         wp_src = wp_words.rearrange("e s p i d -> p (e s) (i d)").bitcast(I32)
@@ -68,9 +68,16 @@ def tile_moe_duo_s_silu_kernel(
         def load_scale_rows(plane, rows, first, r, queue):
             queue.dma_start(out=plane.bitcast(I32)[first + r : P : 32], in_=rows.bitcast(I32)[r])
 
+        def load_scale_run(scales, first, r):
+            rows = scales.rearrange("e s b n -> (e s b) n").bitcast(I32)
+            nc.sync.dma_start(
+                out=s1p[:].bitcast(I32)[first + r : P : 8],
+                in_=rows[r : r + 16 * (E - 1), :].rearrange("(e m) n -> m e n", m=16),
+            )
+
         xs_rows = x_scales.rearrange("s (q r) t -> r q (s t)", r=4)
-        s1_rows = w1_scales.rearrange("e s (q r) n -> r q (e s) n", r=4)
-        sp_rows = wp_scales.rearrange("e s (q r) n -> r q (e s) n", r=4)
+        s1_last = w1_scales[E - 1].rearrange("s (q r) n -> r q (s n)", r=4)
+        sp_last = wp_scales[E - 1].rearrange("s (q r) n -> r q (s n)", r=4)
         s2_rows = w2_scales.rearrange("e s (q r) n -> r q (e s) n", r=4)
 
         nc.sync.dma_start(own_list[:], offs)
@@ -80,20 +87,26 @@ def tile_moe_duo_s_silu_kernel(
         nc.sync.dma_start(out=xw[:], in_=x_words.rearrange("s p t d -> p (s t d)").bitcast(I32))
         nc.scalar.activation(warm_out[:], warm_in[:], SILU)
 
-        for r in range(4):
-            load_scale_rows(s1p[:], sp_rows, 4, r, nc.gpsimd)
+        load_weights(w1, "w1", w1_src, 2 * H, 0, 2, nc.gpsimd)
+        make_identity(nc, ident[:])
         nc.gpsimd.memset(s2[:].bitcast(I32), 0)
-        for r in range(4):
-            load_scale_rows(s2[:], s2_rows, 0, r, nc.gpsimd)
-
+        nc.gpsimd.memset(s1p_last[:].bitcast(I32), 0)
+        small = [(s2[:], s2_rows, 0, r) for r in range(4)]
+        small += [(s1p_last[:], s1_last, 0, r) for r in range(4)] + [(s1p_last[:], sp_last, 4, r) for r in range(4)]
         for j in range(PAIRS):
-            load_weights(wp, "wp", wp_src, 4 * H, 2 * j, 2 * j + 2, nc.sync)
-            load_weights(w1, "w1", w1_src, 2 * H, 2 * j, 2 * j + 2, nc.sync)
             if j == 0:
+                load_weights(wp, "wp", wp_src, 4 * H, 0, 1, nc.sync)
                 for r in range(4):
-                    load_scale_rows(s1p[:], s1_rows, 0, r, nc.sync)
+                    load_scale_run(w1_scales, 0, r)
+                    load_scale_run(wp_scales, 4, r)
+                load_weights(wp, "wp", wp_src, 4 * H, 1, 2, nc.sync)
+            else:
+                load_weights(wp, "wp", wp_src, 4 * H, 2 * j, 2 * j + 2, nc.sync)
+                load_weights(w1, "w1", w1_src, 2 * H, 2 * j, 2 * j + 2, nc.sync)
             if j in W2_AFTER:
                 load_weights(w2, "w2", w2_src, 2 * N, W2_AFTER[j][0], W2_AFTER[j][1], nc.sync)
+            for plane, rows, first, r in small[SMALL_AFTER[j] : SMALL_AFTER[j + 1]]:
+                load_scale_rows(plane, rows, first, r, nc.sync)
 
         x_window = xw[:].bitcast(U32)
         out_view = out.rearrange("(h p) s -> p h s", p=P)
@@ -115,14 +128,15 @@ def tile_moe_duo_s_silu_kernel(
                 gathered.append((words, scales))
             for e in (2 * j, 2 * j + 1):
                 sl = slice((e % 2) * C, (e % 2 + 1) * C)
+                plane = s1p[:, e, :] if e < E - 1 else s1p_last[:]
                 pre = psum.tile([P, H], F32, name="pre_%d" % e, offset=(e % 4) * BANK)
                 nc.tensor.matmul_mx(
                     out=pre[:], lhsT=gathered[0][0][:, sl].bitcast(FP8X4), lhsT_scale=gathered[0][1][:, sl],
-                    rhs=w1[e].bitcast(FP4X4), rhs_scale=s1p[:, e, :], start=True, stop=False,
+                    rhs=w1[e].bitcast(FP4X4), rhs_scale=plane, start=True, stop=False,
                 )
                 nc.tensor.matmul_mx(
                     out=pre[:], lhsT=gathered[1][0][:, sl].bitcast(FP8X4), lhsT_scale=gathered[1][1][:, sl],
-                    rhs=wp[e].bitcast(FP8X4), rhs_scale=s1p[4:P, e, :], start=False, stop=True,
+                    rhs=wp[e].bitcast(FP8X4), rhs_scale=plane[4:P, :], start=False, stop=True,
                 )
                 h = keep.tile([P, H], BF16, name="h_%d" % e, align_bytes=64)
                 nc.scalar.activation(

@@ -19,7 +19,7 @@ SILU = mybir.ActivationFunctionType.Silu
 P = 128
 PAIRS = E // 2
 GROUPS = [(0, 2), (2, 4), (4, 6), (6, 8), (8, 10), (10, 11), (11, 12)]
-W2_AFTER = {3: (0, 2), 4: (2, 4), 5: (4, 12)}
+W2_AFTER = {3: [(0, 2)], 4: [(2, 4)], 5: [(4, 8), (8, 12)]}
 STORE_FROM = {4: 0, 8: 4, 10: 8, 11: 10, 12: 11}
 SMALL_AFTER = [0, 0, 3, 6, 9, 12, 12]
 LAG = 3
@@ -51,7 +51,8 @@ def tile_moe_duo_s_silu_kernel(
         warm_in = keep.tile([P, 1], F32, name="warm_in")
         warm_out = keep.tile([P, 1], F32, name="warm_out")
 
-        nc.gpsimd.memset(xs[:].bitcast(I32), 0)
+        xs_landing = shared.tile([P, LAG * REGION], U8, name="xs_landing", align_bytes=64, offset=REGION)
+        nc.gpsimd.memset(xs_landing[:, 0:T].bitcast(I32), 0)
         nc.gpsimd.memset(warm_in[:], 0.0)
 
         w1_src = w1_words.rearrange("e s p b -> p (e s) b").bitcast(I32)
@@ -80,11 +81,12 @@ def tile_moe_duo_s_silu_kernel(
         sp_last = wp_scales[E - 1].rearrange("s (q r) n -> r q (s n)", r=4)
         s2_rows = w2_scales.rearrange("e s (q r) n -> r q (e s) n", r=4)
 
+        nc.scalar.dma_start(out=xw[:], in_=x_words.rearrange("s p t d -> p (s t d)").bitcast(I32))
         nc.sync.dma_start(own_list[:], offs)
-        for r in range(4):
-            load_scale_rows(xs[:], xs_rows, 0, r, nc.scalar if r < 2 else nc.sync)
         nc.sync.dma_start(partner_list[:], offs2)
-        nc.sync.dma_start(out=xw[:], in_=x_words.rearrange("s p t d -> p (s t d)").bitcast(I32))
+        for r in range(4):
+            load_scale_rows(xs_landing[:, 0:T], xs_rows, 0, r, nc.sync)
+        nc.vector.tensor_copy(xs[:].bitcast(I32), xs_landing[:, 0:T].bitcast(I32))
         nc.scalar.activation(warm_out[:], warm_in[:], SILU)
 
         load_weights(w1, "w1", w1_src, 2 * H, 0, 2, nc.gpsimd)
@@ -103,8 +105,8 @@ def tile_moe_duo_s_silu_kernel(
             else:
                 load_weights(wp, "wp", wp_src, 4 * H, 2 * j, 2 * j + 2, nc.sync)
                 load_weights(w1, "w1", w1_src, 2 * H, 2 * j, 2 * j + 2, nc.sync)
-            if j in W2_AFTER:
-                load_weights(w2, "w2", w2_src, 2 * N, W2_AFTER[j][0], W2_AFTER[j][1], nc.sync)
+            for lo, hi in W2_AFTER.get(j, []):
+                load_weights(w2, "w2", w2_src, 2 * N, lo, hi, nc.sync)
             for plane, rows, first, r in small[SMALL_AFTER[j] : SMALL_AFTER[j + 1]]:
                 load_scale_rows(plane, rows, first, r, nc.sync)
 
@@ -143,6 +145,7 @@ def tile_moe_duo_s_silu_kernel(
                     h[:].rearrange("s (u p d) -> s u p d", u=2, d=2),
                     pre[:].rearrange("s (p u d) -> s u p d", u=2, d=2),
                     SILU,
+                    bias=warm_out[:],
                 )
                 activated[e] = h
 

@@ -17,18 +17,17 @@ FP4X4 = mybir.dt.float4_e2m1fn_x4
 SILU = mybir.ActivationFunctionType.Silu
 
 P = 128
-PAIRS = E // 2
+FIRST = [(0, 1), (1, 3), (3, 5), (5, 7), (7, 9), (9, 11), (11, 12)]
 GROUPS = [(0, 2), (2, 4), (4, 6), (6, 8), (8, 10), (10, 11), (11, 12)]
-W2_AFTER = {3: [(0, 2)], 4: [(2, 4)], 5: [(4, 8), (8, 12)]}
-STORE_FROM = {4: 0, 8: 4, 10: 8, 11: 10, 12: 11}
-SMALL_AFTER = [0, 0, 3, 6, 9, 12, 12]
-LAG = 3
-REGION = 2560
+STORE_FROM = {4: 0, 8: 4, 10: 8, 12: 10}
+LAG = 2
+SLOT = 1024
+QUANTISE_BEFORE = [16, 19, 22, 25, 28, 30, 32, 34]
 BANK = 2048
-TURN_BANK = [2, 0, 2, 0, 2, 4, 5]
-Y_BANK = [6, 7, 6, 7, 1, 3, 0]
-Y_ON_VECTOR = (2, 4, 6)
 TURN_ON_VECTOR = (4,)
+TURN_BANK = [4, 5, 4, 5, 4, 5, 7]
+Y_BANK = [1, 2, 0, 6, 1, 2, 0]
+Y_ON_VECTOR = (3, 5, 6)
 
 
 def tile_moe_duo_s_silu_kernel(
@@ -44,16 +43,12 @@ def tile_moe_duo_s_silu_kernel(
         partner_list = keep.tile([P, E * C // 16], U16, name="partner_list")
         xw = keep.tile([P, T], I32, name="xw", align_bytes=64)
         xs = keep.tile([P, T], U8, name="xs", align_bytes=64)
-        s1p = keep.tile([P, E - 1, H], U8, name="s1p", align_bytes=64)
-        s1p_last = keep.tile([P, H], U8, name="s1p_last", align_bytes=64)
+        s1p = keep.tile([P, E, H], U8, name="s1p", align_bytes=64)
         s2 = keep.tile([P, E, N], U8, name="s2", align_bytes=64)
         ident = keep.tile([P, P], F32, name="ident", align_bytes=64)
         warm_in = keep.tile([P, 1], F32, name="warm_in")
         warm_out = keep.tile([P, 1], F32, name="warm_out")
-
-        xs_landing = shared.tile([P, LAG * REGION], U8, name="xs_landing", align_bytes=64, offset=REGION)
-        nc.gpsimd.memset(xs_landing[:, 0:T].bitcast(I32), 0)
-        nc.gpsimd.memset(warm_in[:], 0.0)
+        xs_landing = shared.tile([P, (QUANTISE_BEFORE[0] - 5) * SLOT], U8, name="xs_landing", align_bytes=64, offset=5 * SLOT)
 
         w1_src = w1_words.rearrange("e s p b -> p (e s) b").bitcast(I32)
         wp_src = wp_words.rearrange("e s p i d -> p (e s) (i d)").bitcast(I32)
@@ -66,49 +61,47 @@ def tile_moe_duo_s_silu_kernel(
             for e in range(lo, hi):
                 store[e] = t[:, e - lo, :]
 
-        def load_scale_rows(plane, rows, first, r, queue):
+        def load_scale_row(plane, rows, first, r, queue):
             queue.dma_start(out=plane.bitcast(I32)[first + r : P : 32], in_=rows.bitcast(I32)[r])
 
-        def load_scale_run(scales, first, r):
-            rows = scales.rearrange("e s b n -> (e s b) n").bitcast(I32)
-            nc.sync.dma_start(
-                out=s1p[:].bitcast(I32)[first + r : P : 8],
-                in_=rows[r : r + 16 * (E - 1), :].rearrange("(e m) n -> m e n", m=16),
-            )
+        def load_scale_rows(plane, rows, first, queue):
+            for r in range(4):
+                load_scale_row(plane, rows, first, r, queue)
 
         xs_rows = x_scales.rearrange("s (q r) t -> r q (s t)", r=4)
-        s1_last = w1_scales[E - 1].rearrange("s (q r) n -> r q (s n)", r=4)
-        sp_last = wp_scales[E - 1].rearrange("s (q r) n -> r q (s n)", r=4)
+        s1_rows = w1_scales.rearrange("e s (q r) n -> r q (e s) n", r=4)
+        sp_rows = wp_scales.rearrange("e s (q r) n -> r q (e s) n", r=4)
         s2_rows = w2_scales.rearrange("e s (q r) n -> r q (e s) n", r=4)
+
+        nc.gpsimd.memset(xs_landing[:, 0:T].bitcast(I32), 0)
+        nc.gpsimd.memset(warm_in[:], 0.0)
+        load_weights(w1, "w1", w1_src, 2 * H, 0, 3, nc.gpsimd)
+        nc.vector.memset(s1p[:].bitcast(I32), 0)
+        nc.gpsimd.memset(s2[:].bitcast(I32), 0)
+        make_identity(nc, ident[:])
 
         nc.scalar.dma_start(out=xw[:], in_=x_words.rearrange("s p t d -> p (s t d)").bitcast(I32))
         nc.sync.dma_start(own_list[:], offs)
         nc.sync.dma_start(partner_list[:], offs2)
-        for r in range(4):
-            load_scale_rows(xs_landing[:, 0:T], xs_rows, 0, r, nc.sync)
+        load_scale_rows(xs_landing[:, 0:T], xs_rows, 0, nc.sync)
         nc.vector.tensor_copy(xs[:].bitcast(I32), xs_landing[:, 0:T].bitcast(I32))
         nc.scalar.activation(warm_out[:], warm_in[:], SILU)
-
-        load_weights(w1, "w1", w1_src, 2 * H, 0, 2, nc.gpsimd)
-        make_identity(nc, ident[:])
-        nc.gpsimd.memset(s2[:].bitcast(I32), 0)
-        nc.gpsimd.memset(s1p_last[:].bitcast(I32), 0)
-        small = [(s2[:], s2_rows, 0, r) for r in range(4)]
-        small += [(s1p_last[:], s1_last, 0, r) for r in range(4)] + [(s1p_last[:], sp_last, 4, r) for r in range(4)]
-        for j in range(PAIRS):
-            if j == 0:
-                load_weights(wp, "wp", wp_src, 4 * H, 0, 1, nc.sync)
-                for r in range(4):
-                    load_scale_run(w1_scales, 0, r)
-                    load_scale_run(wp_scales, 4, r)
-                load_weights(wp, "wp", wp_src, 4 * H, 1, 2, nc.sync)
-            else:
-                load_weights(wp, "wp", wp_src, 4 * H, 2 * j, 2 * j + 2, nc.sync)
-                load_weights(w1, "w1", w1_src, 2 * H, 2 * j, 2 * j + 2, nc.sync)
-            for lo, hi in W2_AFTER.get(j, []):
-                load_weights(w2, "w2", w2_src, 2 * N, lo, hi, nc.sync)
-            for plane, rows, first, r in small[SMALL_AFTER[j] : SMALL_AFTER[j + 1]]:
-                load_scale_rows(plane, rows, first, r, nc.sync)
+        load_weights(wp, "wp", wp_src, 4 * H, 0, 1, nc.scalar)
+        for r in range(4):
+            load_scale_row(s1p[:], s1_rows, 0, r, nc.sync)
+            load_scale_row(s1p[:], sp_rows, 4, r, nc.sync)
+        load_weights(wp, "wp", wp_src, 4 * H, 1, 3, nc.sync)
+        for i in range(2, 5):
+            load_weights(w1, "w1", w1_src, 2 * H, *FIRST[i], nc.sync)
+            load_weights(wp, "wp", wp_src, 4 * H, *FIRST[i], nc.sync)
+            if i == 2:
+                load_scale_rows(s2[:], s2_rows, 0, nc.sync)
+            load_weights(w2, "w2", w2_src, 2 * N, *GROUPS[i - LAG], nc.sync)
+        load_weights(w1, "w1", w1_src, 2 * H, 9, 12, nc.sync)
+        load_weights(w2, "w2", w2_src, 2 * N, 6, 8, nc.sync)
+        load_weights(wp, "wp", wp_src, 4 * H, 9, 11, nc.sync)
+        load_weights(wp, "wp", wp_src, 4 * H, 11, 12, nc.sync)
+        load_weights(w2, "w2", w2_src, 2 * N, 8, 12, nc.sync)
 
         x_window = xw[:].bitcast(U32)
         out_view = out.rearrange("(h p) s -> p h s", p=P)
@@ -116,29 +109,31 @@ def tile_moe_duo_s_silu_kernel(
         grouped = {}
         activated = {}
 
-        def first_layer(j):
-            gathered = []
-            base = j * REGION
-            for name, lst, at_words, at_scales in (("own", own_list, 0, 1024), ("partner", partner_list, 1536, 1280)):
-                words = shared.tile([P, 2 * C], U32, name="%s_words_%d" % (name, j), align_bytes=64, offset=base + at_words)
-                scales = shared.tile([P, 2 * C], U8, name="%s_scales_%d" % (name, j), align_bytes=64, offset=base + at_scales)
-                step = C if (j == PAIRS - 1 and name == "partner") else 2 * C
-                for c0 in range(0, 2 * C, step):
-                    cols = slice((2 * j * C + c0) // 16, (2 * j * C + c0 + step) // 16)
-                    nc.vector.tensor_copy(words[:, c0 : c0 + step], x_window.indirect(lst[:, cols]))
-                    nc.vector.tensor_copy(scales[:, c0 : c0 + step], xs[:].indirect(lst[:, cols]))
-                gathered.append((words, scales))
-            for e in (2 * j, 2 * j + 1):
-                sl = slice((e % 2) * C, (e % 2 + 1) * C)
-                plane = s1p[:, e, :] if e < E - 1 else s1p_last[:]
+        sorts = (
+            (U32, x_window, own_list), (U8, xs[:], own_list), (U32, x_window, partner_list), (U8, xs[:], partner_list)
+        )
+        picked = {}
+
+        def gather(slot):
+            lo, hi = FIRST[slot // 4]
+            dtype, window, lst = sorts[slot % 4]
+            t = shared.tile([P, 2 * C], dtype, name="picked_%d" % slot, align_bytes=64, offset=slot * SLOT)
+            nc.vector.tensor_copy(t[:, 0 : (hi - lo) * C], window.indirect(lst[:, lo * C // 16 : hi * C // 16]))
+            picked[slot] = t
+
+        def first_layer(i):
+            lo, hi = FIRST[i]
+            gathered = [(picked[4 * i], picked[4 * i + 1]), (picked[4 * i + 2], picked[4 * i + 3])]
+            for e in range(lo, hi):
+                sl = slice((e - lo) * C, (e - lo + 1) * C)
                 pre = psum.tile([P, H], F32, name="pre_%d" % e, offset=(e % 4) * BANK)
                 nc.tensor.matmul_mx(
                     out=pre[:], lhsT=gathered[0][0][:, sl].bitcast(FP8X4), lhsT_scale=gathered[0][1][:, sl],
-                    rhs=w1[e].bitcast(FP4X4), rhs_scale=plane, start=True, stop=False,
+                    rhs=w1[e].bitcast(FP4X4), rhs_scale=s1p[:, e, :], start=True, stop=False,
                 )
                 nc.tensor.matmul_mx(
                     out=pre[:], lhsT=gathered[1][0][:, sl].bitcast(FP8X4), lhsT_scale=gathered[1][1][:, sl],
-                    rhs=wp[e].bitcast(FP8X4), rhs_scale=plane[4:P, :], start=False, stop=True,
+                    rhs=wp[e].bitcast(FP8X4), rhs_scale=s1p[4:P, e, :], start=False, stop=True,
                 )
                 h = keep.tile([P, H], BF16, name="h_%d" % e, align_bytes=64)
                 nc.scalar.activation(
@@ -157,10 +152,11 @@ def tile_moe_duo_s_silu_kernel(
                 pairs = activated[e][:].bitcast(F32)
                 for u in range(2):
                     nc.tensor.transpose(turned[:, e - lo, u, :], pairs[:, u * P : (u + 1) * P], ident[:])
-            ht = shared.tile([P, 4 * n], BF16, name="ht_%d" % lo, align_bytes=64, offset=(i + LAG + 1) * REGION + 256)
+            first, last = QUANTISE_BEFORE[i : i + 2]
+            ht = shared.tile([P, (last - first) * SLOT // 2], BF16, name="ht_%d" % lo, align_bytes=64, offset=first * SLOT)
             copy = nc.vector.tensor_copy if i in TURN_ON_VECTOR else nc.scalar.copy
             copy(
-                ht[:].bitcast(F32).rearrange("p (e s u) -> p e s u", u=2, s=C),
+                ht[:, 0 : 4 * n].bitcast(F32).rearrange("p (e s u) -> p e s u", u=2, s=C),
                 turned[:].rearrange("p e u s -> p e s u"),
             )
             grouped[lo] = ht
@@ -170,7 +166,7 @@ def tile_moe_duo_s_silu_kernel(
             n = (hi - lo) * C
             codes = keep.tile([P, n], U32, name="h_codes_%d" % lo, align_bytes=64)
             scales = keep.tile([P, n], U8, name="h_scales_%d" % lo, align_bytes=64)
-            nc.vector.quantize_mx(out=codes[:].bitcast(FP8X4), scales=scales[:], in_=grouped[lo][:])
+            nc.vector.quantize_mx(out=codes[:].bitcast(FP8X4), scales=scales[:], in_=grouped[lo][:, 0 : 4 * n])
             y = psum.tile([P, 2, n], F32, name="y_%d" % lo, offset=Y_BANK[i] * BANK)
             for e in range(lo, hi):
                 sl = slice((e - lo) * C, (e - lo + 1) * C)
@@ -187,10 +183,15 @@ def tile_moe_duo_s_silu_kernel(
                 cols = slice(STORE_FROM[hi] * C, hi * C)
                 nc.sync.dma_start(out=out_view[:, :, cols], in_=staged[:, :, cols])
 
-        for i in range(len(GROUPS) + LAG):
-            if i < PAIRS:
-                first_layer(i)
-            if 1 <= i <= len(GROUPS):
-                turn(i - 1)
-            if i >= LAG:
-                second_layer(i - LAG)
+        for slot in range(4 * len(FIRST)):
+            if slot in QUANTISE_BEFORE:
+                second_layer(QUANTISE_BEFORE.index(slot))
+            gather(slot)
+            if slot % 4 == 3:
+                first_layer(slot // 4)
+                if 1 <= slot // 4 <= 4:
+                    turn(slot // 4 - 1)
+        for i in range(4, 7):
+            turn(i)
+        for i in range(4, 7):
+            second_layer(i)

@@ -18,16 +18,17 @@ SILU = mybir.ActivationFunctionType.Silu
 
 P = 128
 FIRST = [(0, 1), (1, 3), (3, 5), (5, 7), (7, 9), (9, 11), (11, 12)]
-GROUPS = [(0, 2), (2, 4), (4, 6), (6, 8), (8, 10), (10, 11), (11, 12)]
-STORE_FROM = {4: 0, 8: 4, 10: 8, 12: 10}
+GROUPS = [(0, 2), (2, 4), (4, 6), (6, 8), (8, 9), (9, 10), (10, 11), (11, 12)]
+EARLY = 5
+STORE_FROM = {4: 0, 6: 4, 9: 6, 11: 9, 12: 11}
 LAG = 2
 SLOT = 1024
-QUANTISE_BEFORE = [16, 19, 22, 25, 28, 30, 32, 34]
+QUANTISE_BEFORE = [16, 19, 22, 25, 28, 30, 32, 34, 36]
 BANK = 2048
-TURN_ON_VECTOR = (4,)
-TURN_BANK = [4, 5, 4, 5, 4, 5, 7]
-Y_BANK = [1, 2, 0, 6, 1, 2, 0]
-Y_ON_VECTOR = (3, 5, 6)
+TURN_ON_VECTOR = (5,)
+TURN_BANK = [4, 5, 4, 5, 4, 5, 7, 4]
+Y_BANK = [1, 2, 0, 2, 6, 1, 0, 3]
+Y_ON_VECTOR = (3, 6)
 
 
 def tile_moe_duo_s_silu_kernel(
@@ -43,7 +44,8 @@ def tile_moe_duo_s_silu_kernel(
         partner_list = keep.tile([P, E * C // 16], U16, name="partner_list")
         xw = keep.tile([P, T], I32, name="xw", align_bytes=64)
         xs = keep.tile([P, T], U8, name="xs", align_bytes=64)
-        s1p = keep.tile([P, E, H], U8, name="s1p", align_bytes=64)
+        early = keep.tile([P, EARLY, H], U8, name="early", align_bytes=64)
+        late = keep.tile([P, E - EARLY, H], U8, name="late", align_bytes=64)
         s2 = keep.tile([P, E, N], U8, name="s2", align_bytes=64)
         ident = keep.tile([P, P], F32, name="ident", align_bytes=64)
         warm_in = keep.tile([P, 1], F32, name="warm_in")
@@ -76,7 +78,9 @@ def tile_moe_duo_s_silu_kernel(
         nc.gpsimd.memset(xs_landing[:, 0:T].bitcast(I32), 0)
         nc.gpsimd.memset(warm_in[:], 0.0)
         load_weights(w1, "w1", w1_src, 2 * H, 0, 3, nc.gpsimd)
-        nc.vector.memset(s1p[:].bitcast(I32), 0)
+        load_weights(wp, "wp", wp_src, 4 * H, 1, 3, nc.gpsimd)
+        nc.vector.memset(early[:].bitcast(I32), 0)
+        nc.vector.memset(late[:].bitcast(I32), 0)
         nc.gpsimd.memset(s2[:].bitcast(I32), 0)
         make_identity(nc, ident[:])
 
@@ -85,23 +89,23 @@ def tile_moe_duo_s_silu_kernel(
         nc.sync.dma_start(partner_list[:], offs2)
         load_scale_rows(xs_landing[:, 0:T], xs_rows, 0, nc.sync)
         nc.vector.tensor_copy(xs[:].bitcast(I32), xs_landing[:, 0:T].bitcast(I32))
-        nc.scalar.activation(warm_out[:], warm_in[:], SILU)
         load_weights(wp, "wp", wp_src, 4 * H, 0, 1, nc.scalar)
-        for r in range(4):
-            load_scale_row(s1p[:], s1_rows, 0, r, nc.sync)
-            load_scale_row(s1p[:], sp_rows, 4, r, nc.sync)
-        load_weights(wp, "wp", wp_src, 4 * H, 1, 3, nc.sync)
-        for i in range(2, 5):
-            load_weights(w1, "w1", w1_src, 2 * H, *FIRST[i], nc.sync)
-            load_weights(wp, "wp", wp_src, 4 * H, *FIRST[i], nc.sync)
-            if i == 2:
-                load_scale_rows(s2[:], s2_rows, 0, nc.sync)
-            load_weights(w2, "w2", w2_src, 2 * N, *GROUPS[i - LAG], nc.sync)
+        nc.scalar.activation(warm_out[:], warm_in[:], SILU)
+        for plane, lo, hi, step in ((early, 0, EARLY, 2), (late, EARLY, E, 3)):
+            for r in range(4):
+                load_scale_row(plane[:], s1_rows[:, :, lo:hi, :], 0, r, nc.sync)
+                load_scale_row(plane[:], sp_rows[:, :, lo:hi, :], 4, r, nc.sync)
+            load_weights(w1, "w1", w1_src, 2 * H, *FIRST[step], nc.sync)
+            load_weights(wp, "wp", wp_src, 4 * H, *FIRST[step], nc.sync)
+        load_scale_rows(s2[:], s2_rows, 0, nc.sync)
+        load_weights(w2, "w2", w2_src, 2 * N, 0, 4, nc.sync)
+        load_weights(w1, "w1", w1_src, 2 * H, *FIRST[4], nc.sync)
+        load_weights(wp, "wp", wp_src, 4 * H, *FIRST[4], nc.sync)
+        load_weights(w2, "w2", w2_src, 2 * N, 4, 9, nc.sync)
         load_weights(w1, "w1", w1_src, 2 * H, 9, 12, nc.sync)
-        load_weights(w2, "w2", w2_src, 2 * N, 6, 8, nc.sync)
-        load_weights(wp, "wp", wp_src, 4 * H, 9, 11, nc.sync)
-        load_weights(wp, "wp", wp_src, 4 * H, 11, 12, nc.sync)
-        load_weights(w2, "w2", w2_src, 2 * N, 8, 12, nc.sync)
+        for e in range(9, 12):
+            load_weights(wp, "wp", wp_src, 4 * H, e, e + 1, nc.sync)
+        load_weights(w2, "w2", w2_src, 2 * N, 9, 12, nc.sync)
 
         x_window = xw[:].bitcast(U32)
         out_view = out.rearrange("(h p) s -> p h s", p=P)
@@ -126,14 +130,15 @@ def tile_moe_duo_s_silu_kernel(
             gathered = [(picked[4 * i], picked[4 * i + 1]), (picked[4 * i + 2], picked[4 * i + 3])]
             for e in range(lo, hi):
                 sl = slice((e - lo) * C, (e - lo + 1) * C)
+                plane, at = (early, e) if e < EARLY else (late, e - EARLY)
                 pre = psum.tile([P, H], F32, name="pre_%d" % e, offset=(e % 4) * BANK)
                 nc.tensor.matmul_mx(
                     out=pre[:], lhsT=gathered[0][0][:, sl].bitcast(FP8X4), lhsT_scale=gathered[0][1][:, sl],
-                    rhs=w1[e].bitcast(FP4X4), rhs_scale=s1p[:, e, :], start=True, stop=False,
+                    rhs=w1[e].bitcast(FP4X4), rhs_scale=plane[:, at, :], start=True, stop=False,
                 )
                 nc.tensor.matmul_mx(
                     out=pre[:], lhsT=gathered[1][0][:, sl].bitcast(FP8X4), lhsT_scale=gathered[1][1][:, sl],
-                    rhs=wp[e].bitcast(FP8X4), rhs_scale=s1p[4:P, e, :], start=False, stop=True,
+                    rhs=wp[e].bitcast(FP8X4), rhs_scale=plane[4:P, at, :], start=False, stop=True,
                 )
                 h = keep.tile([P, H], BF16, name="h_%d" % e, align_bytes=64)
                 nc.scalar.activation(
@@ -191,7 +196,10 @@ def tile_moe_duo_s_silu_kernel(
                 first_layer(slot // 4)
                 if 1 <= slot // 4 <= 4:
                     turn(slot // 4 - 1)
-        for i in range(4, 7):
+                if slot // 4 == 4:
+                    turn(4)
+        second_layer(4)
+        for i in range(5, 8):
             turn(i)
-        for i in range(4, 7):
+        for i in range(5, 8):
             second_layer(i)

@@ -23,12 +23,12 @@ EARLY = 5
 STORE_FROM = {4: 0, 6: 4, 9: 6, 11: 9, 12: 11}
 LAG = 2
 SLOT = 1024
-QUANTISE_BEFORE = [16, 19, 22, 25, 28, 30, 32, 34, 36]
+QUANTISE_BEFORE = [18, 20, 24, 28, 30, 32, 34, 36, 38]
 BANK = 2048
 TURN_ON_VECTOR = (5,)
-TURN_BANK = [4, 5, 4, 5, 4, 5, 7, 4]
-Y_BANK = [1, 2, 0, 2, 6, 1, 0, 3]
-Y_ON_VECTOR = (3, 6)
+TURN_BANK = [4, 5, 4, 5, 4, 5, 4, 5]
+Y_BANK = [6, 7, 6, 7, 0, 1, 2, 3]
+Y_ON_VECTOR = (1, 3, 5, 7)
 
 
 def tile_moe_duo_s_silu_kernel(
@@ -50,7 +50,7 @@ def tile_moe_duo_s_silu_kernel(
         ident = keep.tile([P, P], F32, name="ident", align_bytes=64)
         warm_in = keep.tile([P, 1], F32, name="warm_in")
         warm_out = keep.tile([P, 1], F32, name="warm_out")
-        xs_landing = shared.tile([P, (QUANTISE_BEFORE[0] - 5) * SLOT], U8, name="xs_landing", align_bytes=64, offset=5 * SLOT)
+        xs_landing = shared.tile([P, (QUANTISE_BEFORE[0] - 8) * SLOT], U8, name="xs_landing", align_bytes=64, offset=8 * SLOT)
 
         w1_src = w1_words.rearrange("e s p b -> p (e s) b").bitcast(I32)
         wp_src = wp_words.rearrange("e s p i d -> p (e s) (i d)").bitcast(I32)
@@ -78,11 +78,10 @@ def tile_moe_duo_s_silu_kernel(
         nc.gpsimd.memset(xs_landing[:, 0:T].bitcast(I32), 0)
         nc.gpsimd.memset(warm_in[:], 0.0)
         load_weights(w1, "w1", w1_src, 2 * H, 0, 3, nc.gpsimd)
-        load_weights(wp, "wp", wp_src, 4 * H, 1, 3, nc.gpsimd)
         nc.vector.memset(early[:].bitcast(I32), 0)
         nc.vector.memset(late[:].bitcast(I32), 0)
-        nc.gpsimd.memset(s2[:].bitcast(I32), 0)
         make_identity(nc, ident[:])
+        nc.gpsimd.memset(s2[:].bitcast(I32), 0)
 
         nc.scalar.dma_start(out=xw[:], in_=x_words.rearrange("s p t d -> p (s t d)").bitcast(I32))
         nc.sync.dma_start(own_list[:], offs)
@@ -91,20 +90,24 @@ def tile_moe_duo_s_silu_kernel(
         nc.vector.tensor_copy(xs[:].bitcast(I32), xs_landing[:, 0:T].bitcast(I32))
         load_weights(wp, "wp", wp_src, 4 * H, 0, 1, nc.scalar)
         nc.scalar.activation(warm_out[:], warm_in[:], SILU)
-        for plane, lo, hi, step in ((early, 0, EARLY, 2), (late, EARLY, E, 3)):
-            for r in range(4):
-                load_scale_row(plane[:], s1_rows[:, :, lo:hi, :], 0, r, nc.sync)
-                load_scale_row(plane[:], sp_rows[:, :, lo:hi, :], 4, r, nc.sync)
-            load_weights(w1, "w1", w1_src, 2 * H, *FIRST[step], nc.sync)
-            load_weights(wp, "wp", wp_src, 4 * H, *FIRST[step], nc.sync)
+        load_scale_rows(early[:], s1_rows[:, :, 0:EARLY, :], 0, nc.sync)
+        load_scale_rows(early[:], sp_rows[:, :, 0:EARLY, :], 4, nc.scalar)
+        load_weights(wp, "wp", wp_src, 4 * H, 1, 3, nc.sync)
+        load_weights(w1, "w1", w1_src, 2 * H, 3, 7, nc.sync)
+        load_weights(wp, "wp", wp_src, 4 * H, 3, 5, nc.sync)
+        load_scale_rows(late[:], s1_rows[:, :, EARLY:E, :], 0, nc.sync)
+        load_weights(wp, "wp", wp_src, 4 * H, 5, 7, nc.sync)
+        load_scale_rows(late[:], sp_rows[:, :, EARLY:E, :], 4, nc.sync)
+        load_weights(w1, "w1", w1_src, 2 * H, 7, 9, nc.sync)
         load_scale_rows(s2[:], s2_rows, 0, nc.sync)
+        load_weights(wp, "wp", wp_src, 4 * H, 7, 9, nc.sync)
         load_weights(w2, "w2", w2_src, 2 * N, 0, 4, nc.sync)
-        load_weights(w1, "w1", w1_src, 2 * H, *FIRST[4], nc.sync)
-        load_weights(wp, "wp", wp_src, 4 * H, *FIRST[4], nc.sync)
-        load_weights(w2, "w2", w2_src, 2 * N, 4, 9, nc.sync)
         load_weights(w1, "w1", w1_src, 2 * H, 9, 12, nc.sync)
-        for e in range(9, 12):
-            load_weights(wp, "wp", wp_src, 4 * H, e, e + 1, nc.sync)
+        load_weights(wp, "wp", wp_src, 4 * H, 9, 10, nc.sync)
+        load_weights(wp, "wp", wp_src, 4 * H, 10, 11, nc.sync)
+        load_weights(w2, "w2", w2_src, 2 * N, 4, 6, nc.sync)
+        load_weights(wp, "wp", wp_src, 4 * H, 11, 12, nc.sync)
+        load_weights(w2, "w2", w2_src, 2 * N, 6, 9, nc.sync)
         load_weights(w2, "w2", w2_src, 2 * N, 9, 12, nc.sync)
 
         x_window = xw[:].bitcast(U32)
@@ -166,12 +169,20 @@ def tile_moe_duo_s_silu_kernel(
             )
             grouped[lo] = ht
 
-        def second_layer(i):
+        quantised = {}
+
+        def quantise(i):
             lo, hi = GROUPS[i]
             n = (hi - lo) * C
             codes = keep.tile([P, n], U32, name="h_codes_%d" % lo, align_bytes=64)
             scales = keep.tile([P, n], U8, name="h_scales_%d" % lo, align_bytes=64)
             nc.vector.quantize_mx(out=codes[:].bitcast(FP8X4), scales=scales[:], in_=grouped[lo][:, 0 : 4 * n])
+            quantised[i] = (codes, scales)
+
+        def second_layer(i):
+            lo, hi = GROUPS[i]
+            n = (hi - lo) * C
+            codes, scales = quantised[i]
             y = psum.tile([P, 2, n], F32, name="y_%d" % lo, offset=Y_BANK[i] * BANK)
             for e in range(lo, hi):
                 sl = slice((e - lo) * C, (e - lo + 1) * C)
@@ -190,16 +201,26 @@ def tile_moe_duo_s_silu_kernel(
 
         for slot in range(4 * len(FIRST)):
             if slot in QUANTISE_BEFORE:
-                second_layer(QUANTISE_BEFORE.index(slot))
+                quantise(QUANTISE_BEFORE.index(slot))
             gather(slot)
             if slot % 4 == 3:
                 first_layer(slot // 4)
+                if slot // 4 == 4:
+                    second_layer(0)
                 if 1 <= slot // 4 <= 4:
                     turn(slot // 4 - 1)
                 if slot // 4 == 4:
                     turn(4)
+            if slot in (20, 24):
+                second_layer(slot // 4 - 4)
+        for i in range(3, 5):
+            quantise(i)
+        turn(5)
+        turn(6)
+        second_layer(3)
+        turn(7)
         second_layer(4)
         for i in range(5, 8):
-            turn(i)
+            quantise(i)
         for i in range(5, 8):
             second_layer(i)

@@ -46,6 +46,7 @@ def tile_moe_duo_s_silu_kernel(
         xs = keep.tile([P, T], U8, name="xs", align_bytes=64)
         early = keep.tile([P, EARLY, H], U8, name="early", align_bytes=64)
         late = keep.tile([P, E - EARLY, H], U8, name="late", align_bytes=64)
+        packed = [keep.tile([P, H], U8, name="packed_%d" % g, align_bytes=64) for g in range(3)]
         s2 = keep.tile([P, E, N], U8, name="s2", align_bytes=64)
         ident = keep.tile([P, P], F32, name="ident", align_bytes=64)
         warm_in = keep.tile([P, 1], F32, name="warm_in")
@@ -70,18 +71,29 @@ def tile_moe_duo_s_silu_kernel(
             for r in range(4):
                 load_scale_row(plane, rows, first, r, queue)
 
+        def load_packed(g, queue):
+            for q in range(4):
+                queue.dma_start(
+                    out=packed[g][:].bitcast(I32)[32 * q : 32 * q + 16],
+                    in_=wp_scales.bitcast(I32)[4 * g : 4 * g + 4, 0, 4 * q : 4 * q + 4, :],
+                )
+
         xs_rows = x_scales.rearrange("s (q r) t -> r q (s t)", r=4)
         s1_rows = w1_scales.rearrange("e s (q r) n -> r q (e s) n", r=4)
-        sp_rows = wp_scales.rearrange("e s (q r) n -> r q (e s) n", r=4)
         s2_rows = w2_scales.rearrange("e s (q r) n -> r q (e s) n", r=4)
 
         nc.gpsimd.memset(xs_landing[:, 0:T].bitcast(I32), 0)
         nc.gpsimd.memset(warm_in[:], 0.0)
         load_weights(w1, "w1", w1_src, 2 * H, 0, 3, nc.gpsimd)
         nc.vector.memset(early[:].bitcast(I32), 0)
+        for g in range(3):
+            nc.vector.memset(packed[g][:].bitcast(I32), 0)
         nc.vector.memset(late[:].bitcast(I32), 0)
+        nc.vector.memset(s2[:].bitcast(I32), 0)
         make_identity(nc, ident[:])
-        nc.gpsimd.memset(s2[:].bitcast(I32), 0)
+        load_scale_rows(late[:], s1_rows[:, :, EARLY:E, :], 0, nc.gpsimd)
+        for r in (2, 3):
+            load_scale_row(s2[:], s2_rows, 0, r, nc.gpsimd)
 
         nc.scalar.dma_start(out=xw[:], in_=x_words.rearrange("s p t d -> p (s t d)").bitcast(I32))
         nc.sync.dma_start(own_list[:], offs)
@@ -91,18 +103,19 @@ def tile_moe_duo_s_silu_kernel(
         load_weights(wp, "wp", wp_src, 4 * H, 0, 1, nc.scalar)
         nc.scalar.activation(warm_out[:], warm_in[:], SILU)
         load_scale_rows(early[:], s1_rows[:, :, 0:EARLY, :], 0, nc.sync)
-        load_scale_rows(early[:], sp_rows[:, :, 0:EARLY, :], 4, nc.scalar)
+        load_packed(0, nc.scalar)
         load_weights(wp, "wp", wp_src, 4 * H, 1, 3, nc.sync)
+        load_packed(1, nc.sync)
         load_weights(w1, "w1", w1_src, 2 * H, 3, 7, nc.sync)
         load_weights(wp, "wp", wp_src, 4 * H, 3, 5, nc.sync)
-        load_scale_rows(late[:], s1_rows[:, :, EARLY:E, :], 0, nc.sync)
+        load_packed(2, nc.sync)
         load_weights(wp, "wp", wp_src, 4 * H, 5, 7, nc.sync)
-        load_scale_rows(late[:], sp_rows[:, :, EARLY:E, :], 4, nc.sync)
         load_weights(w1, "w1", w1_src, 2 * H, 7, 9, nc.sync)
-        load_scale_rows(s2[:], s2_rows, 0, nc.sync)
+        for r in (0, 1):
+            load_scale_row(s2[:], s2_rows, 0, r, nc.sync)
         load_weights(wp, "wp", wp_src, 4 * H, 7, 9, nc.sync)
-        load_weights(w2, "w2", w2_src, 2 * N, 0, 4, nc.sync)
         load_weights(w1, "w1", w1_src, 2 * H, 9, 12, nc.sync)
+        load_weights(w2, "w2", w2_src, 2 * N, 0, 4, nc.sync)
         load_weights(wp, "wp", wp_src, 4 * H, 9, 10, nc.sync)
         load_weights(wp, "wp", wp_src, 4 * H, 10, 11, nc.sync)
         load_weights(w2, "w2", w2_src, 2 * N, 4, 6, nc.sync)
@@ -141,7 +154,7 @@ def tile_moe_duo_s_silu_kernel(
                 )
                 nc.tensor.matmul_mx(
                     out=pre[:], lhsT=gathered[1][0][:, sl].bitcast(FP8X4), lhsT_scale=gathered[1][1][:, sl],
-                    rhs=wp[e].bitcast(FP8X4), rhs_scale=plane[4:P, at, :], start=False, stop=True,
+                    rhs=wp[e].bitcast(FP8X4), rhs_scale=packed[e // 4][4 * (e % 4) : P, :], start=False, stop=True,
                 )
                 h = keep.tile([P, H], BF16, name="h_%d" % e, align_bytes=64)
                 nc.scalar.activation(
@@ -205,12 +218,11 @@ def tile_moe_duo_s_silu_kernel(
             gather(slot)
             if slot % 4 == 3:
                 first_layer(slot // 4)
-                if slot // 4 == 4:
-                    second_layer(0)
                 if 1 <= slot // 4 <= 4:
                     turn(slot // 4 - 1)
                 if slot // 4 == 4:
                     turn(4)
+                    second_layer(0)
             if slot in (20, 24):
                 second_layer(slot // 4 - 4)
         for i in range(3, 5):

@@ -21,7 +21,6 @@ FIRST = [(0, 1), (1, 3), (3, 5), (5, 7), (7, 9), (9, 11), (11, 12)]
 GROUPS = [(0, 2), (2, 4), (4, 6), (6, 8), (8, 9), (9, 10), (10, 11), (11, 12)]
 EARLY = 5
 STORE_FROM = {4: 0, 6: 4, 9: 6, 11: 9, 12: 11}
-LAG = 2
 SLOT = 1024
 QUANTISE_BEFORE = [18, 20, 24, 28, 30, 32, 34, 36, 38]
 BANK = 2048
@@ -51,7 +50,7 @@ def tile_moe_duo_s_silu_kernel(
         ident = keep.tile([P, P], F32, name="ident", align_bytes=64)
         warm_in = keep.tile([P, 1], F32, name="warm_in")
         warm_out = keep.tile([P, 1], F32, name="warm_out")
-        xs_landing = shared.tile([P, (QUANTISE_BEFORE[0] - 8) * SLOT], U8, name="xs_landing", align_bytes=64, offset=8 * SLOT)
+        xs_landing = shared.tile([P, (QUANTISE_BEFORE[0] - 4) * SLOT], U8, name="xs_landing", align_bytes=64, offset=4 * SLOT)
 
         w1_src = w1_words.rearrange("e s p b -> p (e s) b").bitcast(I32)
         wp_src = wp_words.rearrange("e s p i d -> p (e s) (i d)").bitcast(I32)
@@ -82,13 +81,14 @@ def tile_moe_duo_s_silu_kernel(
         s1_rows = w1_scales.rearrange("e s (q r) n -> r q (e s) n", r=4)
         s2_rows = w2_scales.rearrange("e s (q r) n -> r q (e s) n", r=4)
 
-        nc.gpsimd.memset(xs_landing[:, 0:T].bitcast(I32), 0)
-        nc.gpsimd.memset(warm_in[:], 0.0)
         load_weights(w1, "w1", w1_src, 2 * H, 0, 3, nc.gpsimd)
+        nc.vector.memset(xs_landing[:, 0:T].bitcast(I32), 0)
+        nc.vector.memset(packed[0][:].bitcast(I32), 0)
         nc.vector.memset(early[:].bitcast(I32), 0)
-        for g in range(3):
-            nc.vector.memset(packed[g][:].bitcast(I32), 0)
+        nc.vector.memset(warm_in[:], 0.0)
         nc.vector.memset(late[:].bitcast(I32), 0)
+        for g in (1, 2):
+            nc.vector.memset(packed[g][:].bitcast(I32), 0)
         nc.vector.memset(s2[:].bitcast(I32), 0)
         make_identity(nc, ident[:])
         load_scale_rows(late[:], s1_rows[:, :, EARLY:E, :], 0, nc.gpsimd)
@@ -98,16 +98,18 @@ def tile_moe_duo_s_silu_kernel(
         nc.scalar.dma_start(out=xw[:], in_=x_words.rearrange("s p t d -> p (s t d)").bitcast(I32))
         nc.sync.dma_start(own_list[:], offs)
         nc.sync.dma_start(partner_list[:], offs2)
-        load_scale_rows(xs_landing[:, 0:T], xs_rows, 0, nc.sync)
-        nc.vector.tensor_copy(xs[:].bitcast(I32), xs_landing[:, 0:T].bitcast(I32))
+        for r, queue in enumerate((nc.sync, nc.scalar, nc.scalar, nc.sync)):
+            load_scale_row(xs_landing[:, 0:T], xs_rows, 0, r, queue)
         load_weights(wp, "wp", wp_src, 4 * H, 0, 1, nc.scalar)
+        nc.vector.tensor_copy(xs[:].bitcast(I32), xs_landing[:, 0:T].bitcast(I32))
+        load_packed(0, nc.sync)
+        load_scale_rows(early[:], s1_rows[:, :, 0:EARLY, :], 0, nc.scalar)
         nc.scalar.activation(warm_out[:], warm_in[:], SILU)
-        load_scale_rows(early[:], s1_rows[:, :, 0:EARLY, :], 0, nc.sync)
-        load_packed(0, nc.scalar)
         load_weights(wp, "wp", wp_src, 4 * H, 1, 3, nc.sync)
+        load_weights(w1, "w1", w1_src, 2 * H, 3, 5, nc.sync)
         load_packed(1, nc.sync)
-        load_weights(w1, "w1", w1_src, 2 * H, 3, 7, nc.sync)
         load_weights(wp, "wp", wp_src, 4 * H, 3, 5, nc.sync)
+        load_weights(w1, "w1", w1_src, 2 * H, 5, 7, nc.sync)
         load_packed(2, nc.sync)
         load_weights(wp, "wp", wp_src, 4 * H, 5, 7, nc.sync)
         load_weights(w1, "w1", w1_src, 2 * H, 7, 9, nc.sync)
@@ -148,14 +150,16 @@ def tile_moe_duo_s_silu_kernel(
                 sl = slice((e - lo) * C, (e - lo + 1) * C)
                 plane, at = (early, e) if e < EARLY else (late, e - EARLY)
                 pre = psum.tile([P, H], F32, name="pre_%d" % e, offset=(e % 4) * BANK)
-                nc.tensor.matmul_mx(
-                    out=pre[:], lhsT=gathered[0][0][:, sl].bitcast(FP8X4), lhsT_scale=gathered[0][1][:, sl],
-                    rhs=w1[e].bitcast(FP4X4), rhs_scale=plane[:, at, :], start=True, stop=False,
+                moving = (
+                    (w1[e].bitcast(FP4X4), plane[:, at, :]),
+                    (wp[e].bitcast(FP8X4), packed[e // 4][4 * (e % 4) : P, :]),
                 )
-                nc.tensor.matmul_mx(
-                    out=pre[:], lhsT=gathered[1][0][:, sl].bitcast(FP8X4), lhsT_scale=gathered[1][1][:, sl],
-                    rhs=wp[e].bitcast(FP8X4), rhs_scale=packed[e // 4][4 * (e % 4) : P, :], start=False, stop=True,
-                )
+                sides = (1, 0) if e == 0 else (0, 1)
+                for side in sides:
+                    nc.tensor.matmul_mx(
+                        out=pre[:], lhsT=gathered[side][0][:, sl].bitcast(FP8X4), lhsT_scale=gathered[side][1][:, sl],
+                        rhs=moving[side][0], rhs_scale=moving[side][1], start=side == sides[0], stop=side == sides[1],
+                    )
                 h = keep.tile([P, H], BF16, name="h_%d" % e, align_bytes=64)
                 nc.scalar.activation(
                     h[:].rearrange("s (u p d) -> s u p d", u=2, d=2),
@@ -212,7 +216,10 @@ def tile_moe_duo_s_silu_kernel(
                 cols = slice(STORE_FROM[hi] * C, hi * C)
                 nc.sync.dma_start(out=out_view[:, :, cols], in_=staged[:, :, cols])
 
-        for slot in range(4 * len(FIRST)):
+        for slot in (2, 0, 3, 1):
+            gather(slot)
+        first_layer(0)
+        for slot in range(4, 4 * len(FIRST)):
             if slot in QUANTISE_BEFORE:
                 quantise(QUANTISE_BEFORE.index(slot))
             gather(slot)

@@ -20,14 +20,15 @@ P = 128
 FIRST = [(0, 1), (1, 3), (3, 5), (5, 7), (7, 9), (9, 11), (11, 12)]
 GROUPS = [(0, 2), (2, 4), (4, 6), (6, 8), (8, 9), (9, 10), (10, 11), (11, 12)]
 EARLY = 5
-STORE_FROM = {4: 0, 6: 4, 9: 6, 11: 9, 12: 11}
+STORE_FROM = {4: 0, 6: 4, 8: 6, 10: 8, 11: 10, 12: 11}
 SLOT = 1024
-QUANTISE_BEFORE = [18, 20, 24, 28, 30, 32, 34, 36, 38]
+QUANTISE_BEFORE = [18, 20, 22, 28, 30, 32, 34, 36, 38]
 BANK = 2048
-TURN_ON_VECTOR = (5,)
+TURN_ON_VECTOR = (5, 7)
 TURN_BANK = [4, 5, 4, 5, 4, 5, 4, 5]
-Y_BANK = [6, 7, 6, 7, 0, 1, 2, 3]
-Y_ON_VECTOR = (1, 3, 5, 7)
+Y_BANK = [6, 7, 6, 7, 3, 0, 1]
+Y_ON_VECTOR = (2,)
+LAST_BANKS = (2, 4)
 
 
 def tile_moe_duo_s_silu_kernel(
@@ -50,7 +51,7 @@ def tile_moe_duo_s_silu_kernel(
         ident = keep.tile([P, P], F32, name="ident", align_bytes=64)
         warm_in = keep.tile([P, 1], F32, name="warm_in")
         warm_out = keep.tile([P, 1], F32, name="warm_out")
-        xs_landing = shared.tile([P, (QUANTISE_BEFORE[0] - 4) * SLOT], U8, name="xs_landing", align_bytes=64, offset=4 * SLOT)
+        xs_landing = shared.tile([P, (QUANTISE_BEFORE[0] - 5) * SLOT], U8, name="xs_landing", align_bytes=64, offset=5 * SLOT)
 
         w1_src = w1_words.rearrange("e s p b -> p (e s) b").bitcast(I32)
         wp_src = wp_words.rearrange("e s p i d -> p (e s) (i d)").bitcast(I32)
@@ -82,11 +83,11 @@ def tile_moe_duo_s_silu_kernel(
         s2_rows = w2_scales.rearrange("e s (q r) n -> r q (e s) n", r=4)
 
         load_weights(w1, "w1", w1_src, 2 * H, 0, 3, nc.gpsimd)
+        nc.gpsimd.memset(late[:].bitcast(I32), 0)
         nc.vector.memset(xs_landing[:, 0:T].bitcast(I32), 0)
         nc.vector.memset(packed[0][:].bitcast(I32), 0)
         nc.vector.memset(early[:].bitcast(I32), 0)
         nc.vector.memset(warm_in[:], 0.0)
-        nc.vector.memset(late[:].bitcast(I32), 0)
         for g in (1, 2):
             nc.vector.memset(packed[g][:].bitcast(I32), 0)
         nc.vector.memset(s2[:].bitcast(I32), 0)
@@ -116,14 +117,14 @@ def tile_moe_duo_s_silu_kernel(
         for r in (0, 1):
             load_scale_row(s2[:], s2_rows, 0, r, nc.sync)
         load_weights(wp, "wp", wp_src, 4 * H, 7, 9, nc.sync)
-        load_weights(w1, "w1", w1_src, 2 * H, 9, 12, nc.sync)
         load_weights(w2, "w2", w2_src, 2 * N, 0, 4, nc.sync)
-        load_weights(wp, "wp", wp_src, 4 * H, 9, 10, nc.sync)
-        load_weights(wp, "wp", wp_src, 4 * H, 10, 11, nc.sync)
+        load_weights(w1, "w1", w1_src, 2 * H, 9, 11, nc.sync)
         load_weights(w2, "w2", w2_src, 2 * N, 4, 6, nc.sync)
+        load_weights(wp, "wp", wp_src, 4 * H, 9, 11, nc.sync)
+        load_weights(w1, "w1", w1_src, 2 * H, 11, 12, nc.sync)
         load_weights(wp, "wp", wp_src, 4 * H, 11, 12, nc.sync)
-        load_weights(w2, "w2", w2_src, 2 * N, 6, 9, nc.sync)
         load_weights(w2, "w2", w2_src, 2 * N, 9, 12, nc.sync)
+        load_weights(w2, "w2", w2_src, 2 * N, 6, 9, nc.sync)
 
         x_window = xw[:].bitcast(U32)
         out_view = out.rearrange("(h p) s -> p h s", p=P)
@@ -196,6 +197,18 @@ def tile_moe_duo_s_silu_kernel(
             nc.vector.quantize_mx(out=codes[:].bitcast(FP8X4), scales=scales[:], in_=grouped[lo][:, 0 : 4 * n])
             quantised[i] = (codes, scales)
 
+        def product(y, e, half, codes, scales):
+            nc.tensor.matmul_mx(
+                out=y,
+                lhsT=w2[e][:, half * 2 * P : (half + 1) * 2 * P].bitcast(FP4X4),
+                lhsT_scale=s2[:, e, half * P : (half + 1) * P],
+                rhs=codes.bitcast(FP8X4), rhs_scale=scales, start=True, stop=True,
+            )
+
+        def store(hi):
+            cols = slice(STORE_FROM[hi] * C, hi * C)
+            nc.sync.dma_start(out=out_view[:, :, cols], in_=staged[:, :, cols])
+
         def second_layer(i):
             lo, hi = GROUPS[i]
             n = (hi - lo) * C
@@ -204,17 +217,19 @@ def tile_moe_duo_s_silu_kernel(
             for e in range(lo, hi):
                 sl = slice((e - lo) * C, (e - lo + 1) * C)
                 for half in range(2):
-                    nc.tensor.matmul_mx(
-                        out=y[:, half, sl],
-                        lhsT=w2[e][:, half * 2 * P : (half + 1) * 2 * P].bitcast(FP4X4),
-                        lhsT_scale=s2[:, e, half * P : (half + 1) * P],
-                        rhs=codes[:, sl].bitcast(FP8X4), rhs_scale=scales[:, sl], start=True, stop=True,
-                    )
+                    product(y[:, half, sl], e, half, codes[:, sl], scales[:, sl])
             copy = nc.vector.tensor_copy if i in Y_ON_VECTOR else nc.scalar.copy
             copy(staged[:, :, lo * C : hi * C], y[:])
             if hi in STORE_FROM:
-                cols = slice(STORE_FROM[hi] * C, hi * C)
-                nc.sync.dma_start(out=out_view[:, :, cols], in_=staged[:, :, cols])
+                store(hi)
+
+        def last_expert():
+            codes, scales = quantised[len(GROUPS) - 1]
+            for half, copy in enumerate((nc.scalar.copy, nc.vector.tensor_copy)):
+                y = psum.tile([P, C], F32, name="y_last_%d" % half, offset=LAST_BANKS[half] * BANK)
+                product(y[:], E - 1, half, codes[:], scales[:])
+                copy(staged[:, half, (E - 1) * C : E * C], y[:])
+            store(E)
 
         for slot in (2, 0, 3, 1):
             gather(slot)
@@ -230,8 +245,8 @@ def tile_moe_duo_s_silu_kernel(
                 if slot // 4 == 4:
                     turn(4)
                     second_layer(0)
-            if slot in (20, 24):
-                second_layer(slot // 4 - 4)
+            if slot in (20, 22):
+                second_layer(slot // 2 - 9)
         for i in range(3, 5):
             quantise(i)
         turn(5)
@@ -241,5 +256,6 @@ def tile_moe_duo_s_silu_kernel(
         second_layer(4)
         for i in range(5, 8):
             quantise(i)
-        for i in range(5, 8):
+        for i in range(5, 7):
             second_layer(i)
+        last_expert()

@@ -26,9 +26,9 @@ QUANTISE_BEFORE = [18, 20, 22, 28, 30, 32, 34, 36, 38]
 BANK = 2048
 TURN_ON_VECTOR = (5, 7)
 TURN_BANK = [4, 5, 4, 5, 4, 5, 4, 5]
-Y_BANK = [6, 7, 6, 7, 3, 0, 1]
+Y_BANK = [6, 7, 6, 2, 3, 0, 1]
 Y_ON_VECTOR = (2,)
-LAST_BANKS = (2, 4)
+LAST_BANKS = (7, 4)
 
 
 def tile_moe_duo_s_silu_kernel(
@@ -83,16 +83,18 @@ def tile_moe_duo_s_silu_kernel(
         s2_rows = w2_scales.rearrange("e s (q r) n -> r q (e s) n", r=4)
 
         load_weights(w1, "w1", w1_src, 2 * H, 0, 3, nc.gpsimd)
-        nc.gpsimd.memset(late[:].bitcast(I32), 0)
         nc.vector.memset(xs_landing[:, 0:T].bitcast(I32), 0)
         nc.vector.memset(packed[0][:].bitcast(I32), 0)
         nc.vector.memset(early[:].bitcast(I32), 0)
+        load_scale_row(early[:], s1_rows[:, :, 0:EARLY, :], 0, 3, nc.gpsimd)
+        nc.vector.memset(late[:].bitcast(I32), 0)
         nc.vector.memset(warm_in[:], 0.0)
         for g in (1, 2):
             nc.vector.memset(packed[g][:].bitcast(I32), 0)
         nc.vector.memset(s2[:].bitcast(I32), 0)
         make_identity(nc, ident[:])
-        load_scale_rows(late[:], s1_rows[:, :, EARLY:E, :], 0, nc.gpsimd)
+        for r in (0, 1):
+            load_scale_row(late[:], s1_rows[:, :, EARLY:E, :], 0, r, nc.gpsimd)
         for r in (2, 3):
             load_scale_row(s2[:], s2_rows, 0, r, nc.gpsimd)
 
@@ -101,19 +103,22 @@ def tile_moe_duo_s_silu_kernel(
         nc.sync.dma_start(partner_list[:], offs2)
         for r, queue in enumerate((nc.sync, nc.scalar, nc.scalar, nc.sync)):
             load_scale_row(xs_landing[:, 0:T], xs_rows, 0, r, queue)
-        load_weights(wp, "wp", wp_src, 4 * H, 0, 1, nc.scalar)
+        load_weights(wp, "wp", wp_src, 4 * H, 0, 2, nc.scalar)
         nc.vector.tensor_copy(xs[:].bitcast(I32), xs_landing[:, 0:T].bitcast(I32))
         load_packed(0, nc.sync)
-        load_scale_rows(early[:], s1_rows[:, :, 0:EARLY, :], 0, nc.scalar)
+        for r in range(3):
+            load_scale_row(early[:], s1_rows[:, :, 0:EARLY, :], 0, r, nc.scalar)
         nc.scalar.activation(warm_out[:], warm_in[:], SILU)
-        load_weights(wp, "wp", wp_src, 4 * H, 1, 3, nc.sync)
-        load_weights(w1, "w1", w1_src, 2 * H, 3, 5, nc.sync)
-        load_packed(1, nc.sync)
+        load_weights(wp, "wp", wp_src, 4 * H, 2, 3, nc.sync)
         load_weights(wp, "wp", wp_src, 4 * H, 3, 5, nc.sync)
+        load_packed(1, nc.sync)
+        load_weights(w1, "w1", w1_src, 2 * H, 3, 5, nc.sync)
         load_weights(w1, "w1", w1_src, 2 * H, 5, 7, nc.sync)
-        load_packed(2, nc.sync)
+        for r in (2, 3):
+            load_scale_row(late[:], s1_rows[:, :, EARLY:E, :], 0, r, nc.sync)
         load_weights(wp, "wp", wp_src, 4 * H, 5, 7, nc.sync)
         load_weights(w1, "w1", w1_src, 2 * H, 7, 9, nc.sync)
+        load_packed(2, nc.sync)
         for r in (0, 1):
             load_scale_row(s2[:], s2_rows, 0, r, nc.sync)
         load_weights(wp, "wp", wp_src, 4 * H, 7, 9, nc.sync)
@@ -123,8 +128,8 @@ def tile_moe_duo_s_silu_kernel(
         load_weights(wp, "wp", wp_src, 4 * H, 9, 11, nc.sync)
         load_weights(w1, "w1", w1_src, 2 * H, 11, 12, nc.sync)
         load_weights(wp, "wp", wp_src, 4 * H, 11, 12, nc.sync)
-        load_weights(w2, "w2", w2_src, 2 * N, 9, 12, nc.sync)
         load_weights(w2, "w2", w2_src, 2 * N, 6, 9, nc.sync)
+        load_weights(w2, "w2", w2_src, 2 * N, 9, 12, nc.sync)
 
         x_window = xw[:].bitcast(U32)
         out_view = out.rearrange("(h p) s -> p h s", p=P)

@@ -67,10 +67,6 @@ def tile_moe_duo_s_silu_kernel(
         def load_scale_row(plane, rows, first, r, queue):
             queue.dma_start(out=plane.bitcast(I32)[first + r : P : 32], in_=rows.bitcast(I32)[r])
 
-        def load_scale_rows(plane, rows, first, queue):
-            for r in range(4):
-                load_scale_row(plane, rows, first, r, queue)
-
         def load_packed(g, queue):
             for q in range(4):
                 queue.dma_start(
@@ -78,14 +74,13 @@ def tile_moe_duo_s_silu_kernel(
                     in_=wp_scales.bitcast(I32)[4 * g : 4 * g + 4, 0, 4 * q : 4 * q + 4, :],
                 )
 
-        xs_rows = x_scales.rearrange("s (q r) t -> r q (s t)", r=4)
         s1_rows = w1_scales.rearrange("e s (q r) n -> r q (e s) n", r=4)
         s2_rows = w2_scales.rearrange("e s (q r) n -> r q (e s) n", r=4)
 
-        load_weights(w1, "w1", w1_src, 2 * H, 0, 3, nc.gpsimd)
-        nc.vector.memset(xs_landing[:, 0:T].bitcast(I32), 0)
+        load_weights(wp, "wp", wp_src, 4 * H, 0, 2, nc.gpsimd)
         nc.vector.memset(packed[0][:].bitcast(I32), 0)
         nc.vector.memset(early[:].bitcast(I32), 0)
+        nc.vector.memset(xs[:].bitcast(I32), 0)
         load_scale_row(early[:], s1_rows[:, :, 0:EARLY, :], 0, 3, nc.gpsimd)
         nc.vector.memset(late[:].bitcast(I32), 0)
         nc.vector.memset(warm_in[:], 0.0)
@@ -98,17 +93,19 @@ def tile_moe_duo_s_silu_kernel(
         for r in (2, 3):
             load_scale_row(s2[:], s2_rows, 0, r, nc.gpsimd)
 
+        xs_by_quarter = xs_landing[0:4, 0 : 4 * T].bitcast(I32).rearrange("r (q t) -> r q t", q=4)
+        nc.scalar.dma_start(out=xs_by_quarter, in_=x_scales.rearrange("s (q r) t -> r (s q) t", r=4).bitcast(I32))
         nc.scalar.dma_start(out=xw[:], in_=x_words.rearrange("s p t d -> p (s t d)").bitcast(I32))
-        nc.sync.dma_start(own_list[:], offs)
         nc.sync.dma_start(partner_list[:], offs2)
-        for r, queue in enumerate((nc.sync, nc.scalar, nc.scalar, nc.sync)):
-            load_scale_row(xs_landing[:, 0:T], xs_rows, 0, r, queue)
-        load_weights(wp, "wp", wp_src, 4 * H, 0, 2, nc.scalar)
-        nc.vector.tensor_copy(xs[:].bitcast(I32), xs_landing[:, 0:T].bitcast(I32))
+        nc.sync.dma_start(own_list[:], offs)
+        load_weights(w1, "w1", w1_src, 2 * H, 0, 2, nc.scalar)
+        for q in range(4):
+            nc.vector.tensor_copy(xs[:].bitcast(I32)[32 * q : 32 * q + 4], xs_by_quarter[:, q, :])
         load_packed(0, nc.sync)
         for r in range(3):
             load_scale_row(early[:], s1_rows[:, :, 0:EARLY, :], 0, r, nc.scalar)
         nc.scalar.activation(warm_out[:], warm_in[:], SILU)
+        load_weights(w1, "w1", w1_src, 2 * H, 2, 3, nc.sync)
         load_weights(wp, "wp", wp_src, 4 * H, 2, 3, nc.sync)
         load_weights(wp, "wp", wp_src, 4 * H, 3, 5, nc.sync)
         load_packed(1, nc.sync)

@@ -21,11 +21,23 @@ FIRST = [(0, 1), (1, 3), (3, 5), (5, 7), (7, 9), (9, 11), (11, 12)]
 GROUPS = [(0, 2), (2, 4), (4, 6), (6, 8), (8, 9), (9, 10), (10, 11), (11, 12)]
 EARLY = 5
 STORE_FROM = {4: 0, 6: 4, 8: 6, 10: 8, 11: 10, 12: 11}
-SLOT = 1024
-QUANTISE_BEFORE = [18, 20, 22, 28, 30, 32, 34, 36, 38]
+OWN, PARTNER = 0, 1
+WORDS, BYTES = 0, 1
+GATHERS = [
+    [(PARTNER, WORDS, 0, 1), (OWN, WORDS, 0, 1), (PARTNER, BYTES, 0, 1), (OWN, BYTES, 0, 1), (OWN, WORDS, 1, 3)],
+    [(OWN, BYTES, 1, 5), (PARTNER, WORDS, 1, 3), (PARTNER, BYTES, 1, 3),
+     (OWN, WORDS, 3, 5), (PARTNER, BYTES, 3, 7), (PARTNER, WORDS, 3, 5),
+     (OWN, BYTES, 5, 9), (OWN, WORDS, 5, 7), (PARTNER, WORDS, 5, 7),
+     (OWN, WORDS, 7, 9)],
+    [(PARTNER, BYTES, 7, 11), (PARTNER, WORDS, 7, 9)],
+    [(OWN, BYTES, 9, 11), (OWN, WORDS, 9, 11), (PARTNER, WORDS, 9, 11), (OWN, BYTES, 11, 12), (OWN, WORDS, 11, 12), (PARTNER, BYTES, 11, 12), (PARTNER, WORDS, 11, 12)],
+]
+HELD_AT = [6144, 0, 2048]
+LANDING = 10 * 1024
+WINDOW = 768
 BANK = 2048
 TURN_ON_VECTOR = (5, 7)
-TURN_BANK = [4, 5, 4, 5, 4, 5, 4, 5]
+TURN_BANK = [1, 3, 1, 3, 4, 5, 4, 5]
 Y_BANK = [6, 7, 6, 2, 3, 0, 1]
 Y_ON_VECTOR = (2,)
 LAST_BANKS = (7, 4)
@@ -43,7 +55,8 @@ def tile_moe_duo_s_silu_kernel(
         own_list = keep.tile([P, E * C // 16], U16, name="own_list")
         partner_list = keep.tile([P, E * C // 16], U16, name="partner_list")
         xw = keep.tile([P, T], I32, name="xw", align_bytes=64)
-        xs = keep.tile([P, T], U8, name="xs", align_bytes=64)
+        xs = keep.tile([P, WINDOW], U8, name="xs", align_bytes=64)
+        xs_landing = shared.tile([P, LANDING], U8, name="xs_landing", align_bytes=64, offset=HELD_AT[0])
         early = keep.tile([P, EARLY, H], U8, name="early", align_bytes=64)
         late = keep.tile([P, E - EARLY, H], U8, name="late", align_bytes=64)
         packed = [keep.tile([P, H], U8, name="packed_%d" % g, align_bytes=64) for g in range(3)]
@@ -51,7 +64,6 @@ def tile_moe_duo_s_silu_kernel(
         ident = keep.tile([P, P], F32, name="ident", align_bytes=64)
         warm_in = keep.tile([P, 1], F32, name="warm_in")
         warm_out = keep.tile([P, 1], F32, name="warm_out")
-        xs_landing = shared.tile([P, (QUANTISE_BEFORE[0] - 5) * SLOT], U8, name="xs_landing", align_bytes=64, offset=5 * SLOT)
 
         w1_src = w1_words.rearrange("e s p b -> p (e s) b").bitcast(I32)
         wp_src = wp_words.rearrange("e s p i d -> p (e s) (i d)").bitcast(I32)
@@ -74,16 +86,18 @@ def tile_moe_duo_s_silu_kernel(
                     in_=wp_scales.bitcast(I32)[4 * g : 4 * g + 4, 0, 4 * q : 4 * q + 4, :],
                 )
 
+        xs_rows = x_scales.rearrange("s (q r) t -> r q (s t)", r=4)
         s1_rows = w1_scales.rearrange("e s (q r) n -> r q (e s) n", r=4)
         s2_rows = w2_scales.rearrange("e s (q r) n -> r q (e s) n", r=4)
 
-        load_weights(wp, "wp", wp_src, 4 * H, 0, 2, nc.gpsimd)
+        load_weights(w1, "w1", w1_src, 2 * H, 0, 3, nc.gpsimd)
+        nc.vector.memset(xs_landing[:, 0:T].bitcast(I32), 0)
         nc.vector.memset(packed[0][:].bitcast(I32), 0)
         nc.vector.memset(early[:].bitcast(I32), 0)
-        nc.vector.memset(xs[:].bitcast(I32), 0)
         load_scale_row(early[:], s1_rows[:, :, 0:EARLY, :], 0, 3, nc.gpsimd)
         nc.vector.memset(late[:].bitcast(I32), 0)
         nc.vector.memset(warm_in[:], 0.0)
+        nc.vector.memset(xs[:, T:WINDOW].bitcast(I32), 0)
         for g in (1, 2):
             nc.vector.memset(packed[g][:].bitcast(I32), 0)
         nc.vector.memset(s2[:].bitcast(I32), 0)
@@ -93,19 +107,17 @@ def tile_moe_duo_s_silu_kernel(
         for r in (2, 3):
             load_scale_row(s2[:], s2_rows, 0, r, nc.gpsimd)
 
-        xs_by_quarter = xs_landing[0:4, 0 : 4 * T].bitcast(I32).rearrange("r (q t) -> r q t", q=4)
-        nc.scalar.dma_start(out=xs_by_quarter, in_=x_scales.rearrange("s (q r) t -> r (s q) t", r=4).bitcast(I32))
         nc.scalar.dma_start(out=xw[:], in_=x_words.rearrange("s p t d -> p (s t d)").bitcast(I32))
-        nc.sync.dma_start(partner_list[:], offs2)
         nc.sync.dma_start(own_list[:], offs)
-        load_weights(w1, "w1", w1_src, 2 * H, 0, 2, nc.scalar)
-        for q in range(4):
-            nc.vector.tensor_copy(xs[:].bitcast(I32)[32 * q : 32 * q + 4], xs_by_quarter[:, q, :])
+        nc.sync.dma_start(partner_list[:], offs2)
+        for r, queue in enumerate((nc.sync, nc.scalar, nc.scalar, nc.sync)):
+            load_scale_row(xs_landing[:, 0:T], xs_rows, 0, r, queue)
+        load_weights(wp, "wp", wp_src, 4 * H, 0, 2, nc.scalar)
+        nc.vector.tensor_copy(xs[:, 0:T].bitcast(I32), xs_landing[:, 0:T].bitcast(I32))
         load_packed(0, nc.sync)
         for r in range(3):
             load_scale_row(early[:], s1_rows[:, :, 0:EARLY, :], 0, r, nc.scalar)
         nc.scalar.activation(warm_out[:], warm_in[:], SILU)
-        load_weights(w1, "w1", w1_src, 2 * H, 2, 3, nc.sync)
         load_weights(wp, "wp", wp_src, 4 * H, 2, 3, nc.sync)
         load_weights(wp, "wp", wp_src, 4 * H, 3, 5, nc.sync)
         load_packed(1, nc.sync)
@@ -121,12 +133,11 @@ def tile_moe_duo_s_silu_kernel(
         load_weights(wp, "wp", wp_src, 4 * H, 7, 9, nc.sync)
         load_weights(w2, "w2", w2_src, 2 * N, 0, 4, nc.sync)
         load_weights(w1, "w1", w1_src, 2 * H, 9, 11, nc.sync)
-        load_weights(w2, "w2", w2_src, 2 * N, 4, 6, nc.sync)
         load_weights(wp, "wp", wp_src, 4 * H, 9, 11, nc.sync)
         load_weights(w1, "w1", w1_src, 2 * H, 11, 12, nc.sync)
         load_weights(wp, "wp", wp_src, 4 * H, 11, 12, nc.sync)
-        load_weights(w2, "w2", w2_src, 2 * N, 6, 9, nc.sync)
-        load_weights(w2, "w2", w2_src, 2 * N, 9, 12, nc.sync)
+        load_weights(w2, "w2", w2_src, 2 * N, 4, 8, nc.sync)
+        load_weights(w2, "w2", w2_src, 2 * N, 8, 12, nc.sync)
 
         x_window = xw[:].bitcast(U32)
         out_view = out.rearrange("(h p) s -> p h s", p=P)
@@ -134,23 +145,28 @@ def tile_moe_duo_s_silu_kernel(
         grouped = {}
         activated = {}
 
-        sorts = (
-            (U32, x_window, own_list), (U8, xs[:], own_list), (U32, x_window, partner_list), (U8, xs[:], partner_list)
-        )
+        windows = (x_window, xs[:])
+        lists = (own_list, partner_list)
         picked = {}
 
-        def gather(slot):
-            lo, hi = FIRST[slot // 4]
-            dtype, window, lst = sorts[slot % 4]
-            t = shared.tile([P, 2 * C], dtype, name="picked_%d" % slot, align_bytes=64, offset=slot * SLOT)
-            nc.vector.tensor_copy(t[:, 0 : (hi - lo) * C], window.indirect(lst[:, lo * C // 16 : hi * C // 16]))
-            picked[slot] = t
+        def gather(batch):
+            at = HELD_AT[batch - 1] if batch else None
+            for side, sort, lo, hi in GATHERS[batch]:
+                n = (hi - lo) * C
+                dtype, size = ((U32, 4), (U8, 1))[sort]
+                name = "picked_%d_%d_%d" % (side, sort, lo)
+                if batch:
+                    t = shared.tile([P, n], dtype, name=name, align_bytes=64, offset=at)
+                    at = at + n * size
+                else:
+                    t = keep.tile([P, n], dtype, name=name, align_bytes=64)
+                nc.vector.tensor_copy(t[:], windows[sort].indirect(lists[side][:, lo * C // 16 : hi * C // 16]))
+                for e in range(lo, hi):
+                    picked[side, sort, e] = t[:, (e - lo) * C : (e - lo + 1) * C]
 
         def first_layer(i):
             lo, hi = FIRST[i]
-            gathered = [(picked[4 * i], picked[4 * i + 1]), (picked[4 * i + 2], picked[4 * i + 3])]
             for e in range(lo, hi):
-                sl = slice((e - lo) * C, (e - lo + 1) * C)
                 plane, at = (early, e) if e < EARLY else (late, e - EARLY)
                 pre = psum.tile([P, H], F32, name="pre_%d" % e, offset=(e % 4) * BANK)
                 moving = (
@@ -160,7 +176,7 @@ def tile_moe_duo_s_silu_kernel(
                 sides = (1, 0) if e == 0 else (0, 1)
                 for side in sides:
                     nc.tensor.matmul_mx(
-                        out=pre[:], lhsT=gathered[side][0][:, sl].bitcast(FP8X4), lhsT_scale=gathered[side][1][:, sl],
+                        out=pre[:], lhsT=picked[side, WORDS, e].bitcast(FP8X4), lhsT_scale=picked[side, BYTES, e],
                         rhs=moving[side][0], rhs_scale=moving[side][1], start=side == sides[0], stop=side == sides[1],
                     )
                 h = keep.tile([P, H], BF16, name="h_%d" % e, align_bytes=64)
@@ -180,8 +196,10 @@ def tile_moe_duo_s_silu_kernel(
                 pairs = activated[e][:].bitcast(F32)
                 for u in range(2):
                     nc.tensor.transpose(turned[:, e - lo, u, :], pairs[:, u * P : (u + 1) * P], ident[:])
-            first, last = QUANTISE_BEFORE[i : i + 2]
-            ht = shared.tile([P, (last - first) * SLOT // 2], BF16, name="ht_%d" % lo, align_bytes=64, offset=first * SLOT)
+            if i < 2:
+                ht = shared.tile([P, (1024, 2048)[i]], BF16, name="ht_%d" % lo, align_bytes=64, offset=HELD_AT[i + 1])
+            else:
+                ht = keep.tile([P, 4 * n], BF16, name="ht_%d" % lo, align_bytes=64)
             copy = nc.vector.tensor_copy if i in TURN_ON_VECTOR else nc.scalar.copy
             copy(
                 ht[:, 0 : 4 * n].bitcast(F32).rearrange("p (e s u) -> p e s u", u=2, s=C),
@@ -233,24 +251,29 @@ def tile_moe_duo_s_silu_kernel(
                 copy(staged[:, half, (E - 1) * C : E * C], y[:])
             store(E)
 
-        for slot in (2, 0, 3, 1):
-            gather(slot)
+        gather(0)
+        gather(1)
         first_layer(0)
-        for slot in range(4, 4 * len(FIRST)):
-            if slot in QUANTISE_BEFORE:
-                quantise(QUANTISE_BEFORE.index(slot))
-            gather(slot)
-            if slot % 4 == 3:
-                first_layer(slot // 4)
-                if 1 <= slot // 4 <= 4:
-                    turn(slot // 4 - 1)
-                if slot // 4 == 4:
-                    turn(4)
-                    second_layer(0)
-            if slot in (20, 22):
-                second_layer(slot // 2 - 9)
-        for i in range(3, 5):
+        first_layer(1)
+        turn(0)
+        first_layer(2)
+        turn(1)
+        first_layer(3)
+        turn(2)
+        quantise(0)
+        gather(2)
+        first_layer(4)
+        turn(3)
+        turn(4)
+        second_layer(0)
+        quantise(1)
+        gather(3)
+        second_layer(1)
+        first_layer(5)
+        first_layer(6)
+        for i in range(2, 5):
             quantise(i)
+        second_layer(2)
         turn(5)
         turn(6)
         second_layer(3)

@@ -28,15 +28,15 @@ GATHERS = [
     [(OWN, BYTES, 1, 5), (PARTNER, WORDS, 1, 3), (PARTNER, BYTES, 1, 3),
      (OWN, WORDS, 3, 5), (PARTNER, BYTES, 3, 7), (PARTNER, WORDS, 3, 5),
      (OWN, BYTES, 5, 9), (OWN, WORDS, 5, 7), (PARTNER, WORDS, 5, 7),
-     (OWN, WORDS, 7, 9)],
-    [(PARTNER, BYTES, 7, 11), (PARTNER, WORDS, 7, 9)],
-    [(OWN, BYTES, 9, 11), (OWN, WORDS, 9, 11), (PARTNER, WORDS, 9, 11), (OWN, BYTES, 11, 12), (OWN, WORDS, 11, 12), (PARTNER, BYTES, 11, 12), (PARTNER, WORDS, 11, 12)],
+     (OWN, WORDS, 7, 9), (PARTNER, BYTES, 7, 9), (PARTNER, WORDS, 7, 9)],
+    [(OWN, BYTES, 9, 11), (OWN, WORDS, 9, 11), (PARTNER, BYTES, 9, 11), (PARTNER, WORDS, 9, 11),
+     (OWN, BYTES, 11, 12), (OWN, WORDS, 11, 12), (PARTNER, BYTES, 11, 12), (PARTNER, WORDS, 11, 12)],
 ]
-HELD_AT = [6144, 0, 2048]
-LANDING = 10 * 1024
+HELD_AT = [4096, 0]
+LANDING = 11 * 1024
 WINDOW = 768
 BANK = 2048
-TURN_ON_VECTOR = (5, 7)
+TURN_ON_VECTOR = (4, 5, 7)
 TURN_BANK = [1, 3, 1, 3, 4, 5, 4, 5]
 Y_BANK = [6, 7, 6, 2, 3, 0, 1]
 Y_ON_VECTOR = (2,)
@@ -143,6 +143,7 @@ def tile_moe_duo_s_silu_kernel(
         out_view = out.rearrange("(h p) s -> p h s", p=P)
         staged = keep.tile([P, 2, E * C], F32, name="staged")
         grouped = {}
+        first_four = shared.tile([P, 4 * 4 * C], BF16, name="first_four", align_bytes=64, offset=HELD_AT[1])
         activated = {}
 
         windows = (x_window, xs[:])
@@ -197,7 +198,7 @@ def tile_moe_duo_s_silu_kernel(
                 for u in range(2):
                     nc.tensor.transpose(turned[:, e - lo, u, :], pairs[:, u * P : (u + 1) * P], ident[:])
             if i < 2:
-                ht = shared.tile([P, (1024, 2048)[i]], BF16, name="ht_%d" % lo, align_bytes=64, offset=HELD_AT[i + 1])
+                ht = first_four[:, 4 * lo * C : 4 * hi * C]
             else:
                 ht = keep.tile([P, 4 * n], BF16, name="ht_%d" % lo, align_bytes=64)
             copy = nc.vector.tensor_copy if i in TURN_ON_VECTOR else nc.scalar.copy
@@ -216,6 +217,13 @@ def tile_moe_duo_s_silu_kernel(
             scales = keep.tile([P, n], U8, name="h_scales_%d" % lo, align_bytes=64)
             nc.vector.quantize_mx(out=codes[:].bitcast(FP8X4), scales=scales[:], in_=grouped[lo][:, 0 : 4 * n])
             quantised[i] = (codes, scales)
+
+        def quantise_first_four():
+            codes = keep.tile([P, 4 * C], U32, name="h_codes_first", align_bytes=64)
+            scales = keep.tile([P, 4 * C], U8, name="h_scales_first", align_bytes=64)
+            nc.vector.quantize_mx(out=codes[:].bitcast(FP8X4), scales=scales[:], in_=first_four[:])
+            for i in range(2):
+                quantised[i] = (codes[:, 2 * C * i : 2 * C * (i + 1)], scales[:, 2 * C * i : 2 * C * (i + 1)])
 
         def product(y, e, half, codes, scales):
             nc.tensor.matmul_mx(
@@ -260,19 +268,18 @@ def tile_moe_duo_s_silu_kernel(
         turn(1)
         first_layer(3)
         turn(2)
-        quantise(0)
+        quantise_first_four()
         gather(2)
         first_layer(4)
         turn(3)
-        turn(4)
         second_layer(0)
-        quantise(1)
-        gather(3)
         second_layer(1)
         first_layer(5)
         first_layer(6)
-        for i in range(2, 5):
-            quantise(i)
+        quantise(2)
+        quantise(3)
+        turn(4)
+        quantise(4)
         second_layer(2)
         turn(5)
         turn(6)

from contextlib import ExitStack

import concourse.mybir as mybir
from concourse.masks import make_identity

K, T, E, C, H, N = 512, 512, 12, 128, 512, 256
FLOPS = 2 * E * C * (2 * K * H + H * N)

F32 = mybir.dt.float32
BF16 = mybir.dt.bfloat16
I32 = mybir.dt.int32
U32 = mybir.dt.uint32
U16 = mybir.dt.uint16
U8 = mybir.dt.uint8
FP8X4 = mybir.dt.float8_e4m3fn_x4
FP4X4 = mybir.dt.float4_e2m1fn_x4
SILU = mybir.ActivationFunctionType.Silu

P = 128
FIRST = [(0, 1), (1, 3), (3, 5), (5, 7), (7, 9), (9, 11), (11, 12)]
GROUPS = [(0, 2), (2, 4), (4, 6), (6, 8), (8, 9), (9, 10), (10, 11), (11, 12)]
EARLY = 5
STORE_FROM = {4: 0, 6: 4, 8: 6, 10: 8, 11: 10, 12: 11}
OWN, PARTNER = 0, 1
WORDS, BYTES = 0, 1
GATHERS = [
    [(PARTNER, WORDS, 0, 1), (OWN, WORDS, 0, 1), (PARTNER, BYTES, 0, 1), (OWN, BYTES, 0, 1), (OWN, WORDS, 1, 3)],
    [(OWN, BYTES, 1, 5), (PARTNER, WORDS, 1, 3), (PARTNER, BYTES, 1, 3),
     (OWN, WORDS, 3, 5), (PARTNER, BYTES, 3, 7), (PARTNER, WORDS, 3, 5),
     (OWN, BYTES, 5, 9), (OWN, WORDS, 5, 7), (PARTNER, WORDS, 5, 7),
     (OWN, WORDS, 7, 9), (PARTNER, BYTES, 7, 9), (PARTNER, WORDS, 7, 9)],
    [(OWN, BYTES, 9, 11), (OWN, WORDS, 9, 11), (PARTNER, BYTES, 9, 11), (PARTNER, WORDS, 9, 11),
     (OWN, BYTES, 11, 12), (OWN, WORDS, 11, 12), (PARTNER, BYTES, 11, 12), (PARTNER, WORDS, 11, 12)],
]
HELD_AT = [4096, 0]
LANDING = 11 * 1024
WINDOW = 768
BANK = 2048
TURN_ON_VECTOR = (4, 5, 7)
TURN_BANK = [1, 3, 1, 3, 4, 5, 4, 5]
Y_BANK = [6, 7, 6, 2, 3, 0, 1]
Y_ON_VECTOR = (2,)
LAST_BANKS = (7, 4)


def tile_moe_duo_s_silu_kernel(
    tc, x_words, x_scales, w1_words, w1_scales, wp_words, wp_scales, w2_words, w2_scales, offs, offs2, out
):
    nc = tc.nc
    with ExitStack() as ctx:
        keep = ctx.enter_context(tc.tile_pool(name="keep", bufs=1))
        shared = ctx.enter_context(tc.tile_pool(name="shared", bufs=1))
        psum = ctx.enter_context(tc.psum_pool(name="psum", bufs=1))

        own_list = keep.tile([P, E * C // 16], U16, name="own_list")
        partner_list = keep.tile([P, E * C // 16], U16, name="partner_list")
        xw = keep.tile([P, T], I32, name="xw", align_bytes=64)
        xs = keep.tile([P, WINDOW], U8, name="xs", align_bytes=64)
        xs_landing = shared.tile([P, LANDING], U8, name="xs_landing", align_bytes=64, offset=HELD_AT[0])
        early = keep.tile([P, EARLY, H], U8, name="early", align_bytes=64)
        late = keep.tile([P, E - EARLY, H], U8, name="late", align_bytes=64)
        packed = [keep.tile([P, H], U8, name="packed_%d" % g, align_bytes=64) for g in range(3)]
        s2 = keep.tile([P, E, N], U8, name="s2", align_bytes=64)
        ident = keep.tile([P, P], F32, name="ident", align_bytes=64)
        warm_in = keep.tile([P, 1], F32, name="warm_in")
        warm_out = keep.tile([P, 1], F32, name="warm_out")

        w1_src = w1_words.rearrange("e s p b -> p (e s) b").bitcast(I32)
        wp_src = wp_words.rearrange("e s p i d -> p (e s) (i d)").bitcast(I32)
        w2_src = w2_words.rearrange("e s p b -> p (e s) b").bitcast(I32)
        w1, wp, w2 = {}, {}, {}

        def load_weights(store, name, src, width, lo, hi, queue):
            t = keep.tile([P, hi - lo, width], U8, name="%s_%d" % (name, lo), align_bytes=64)
            queue.dma_start(out=t[:].bitcast(I32), in_=src[:, lo:hi, :])
            for e in range(lo, hi):
                store[e] = t[:, e - lo, :]

        def load_scale_row(plane, rows, first, r, queue):
            queue.dma_start(out=plane.bitcast(I32)[first + r : P : 32], in_=rows.bitcast(I32)[r])

        def load_packed(g, queue):
            for q in range(4):
                queue.dma_start(
                    out=packed[g][:].bitcast(I32)[32 * q : 32 * q + 16],
                    in_=wp_scales.bitcast(I32)[4 * g : 4 * g + 4, 0, 4 * q : 4 * q + 4, :],
                )

        xs_rows = x_scales.rearrange("s (q r) t -> r q (s t)", r=4)
        s1_rows = w1_scales.rearrange("e s (q r) n -> r q (e s) n", r=4)
        s2_rows = w2_scales.rearrange("e s (q r) n -> r q (e s) n", r=4)

        load_weights(w1, "w1", w1_src, 2 * H, 0, 3, nc.gpsimd)
        nc.vector.memset(xs_landing[:, 0:T].bitcast(I32), 0)
        nc.vector.memset(packed[0][:].bitcast(I32), 0)
        nc.vector.memset(early[:].bitcast(I32), 0)
        load_scale_row(early[:], s1_rows[:, :, 0:EARLY, :], 0, 3, nc.gpsimd)
        nc.vector.memset(late[:].bitcast(I32), 0)
        nc.vector.memset(warm_in[:], 0.0)
        nc.vector.memset(xs[:, T:WINDOW].bitcast(I32), 0)
        for g in (1, 2):
            nc.vector.memset(packed[g][:].bitcast(I32), 0)
        nc.vector.memset(s2[:].bitcast(I32), 0)
        make_identity(nc, ident[:])
        for r in (0, 1):
            load_scale_row(late[:], s1_rows[:, :, EARLY:E, :], 0, r, nc.gpsimd)
        for r in (2, 3):
            load_scale_row(s2[:], s2_rows, 0, r, nc.gpsimd)

        nc.scalar.dma_start(out=xw[:], in_=x_words.rearrange("s p t d -> p (s t d)").bitcast(I32))
        nc.sync.dma_start(own_list[:], offs)
        nc.sync.dma_start(partner_list[:], offs2)
        for r, queue in enumerate((nc.sync, nc.scalar, nc.scalar, nc.sync)):
            load_scale_row(xs_landing[:, 0:T], xs_rows, 0, r, queue)
        load_weights(wp, "wp", wp_src, 4 * H, 0, 2, nc.scalar)
        nc.vector.tensor_copy(xs[:, 0:T].bitcast(I32), xs_landing[:, 0:T].bitcast(I32))
        load_packed(0, nc.sync)
        for r in range(3):
            load_scale_row(early[:], s1_rows[:, :, 0:EARLY, :], 0, r, nc.scalar)
        nc.scalar.activation(warm_out[:], warm_in[:], SILU)
        load_weights(wp, "wp", wp_src, 4 * H, 2, 3, nc.sync)
        load_weights(wp, "wp", wp_src, 4 * H, 3, 5, nc.sync)
        load_packed(1, nc.sync)
        load_weights(w1, "w1", w1_src, 2 * H, 3, 5, nc.sync)
        load_weights(w1, "w1", w1_src, 2 * H, 5, 7, nc.sync)
        for r in (2, 3):
            load_scale_row(late[:], s1_rows[:, :, EARLY:E, :], 0, r, nc.sync)
        load_weights(wp, "wp", wp_src, 4 * H, 5, 7, nc.sync)
        load_weights(w1, "w1", w1_src, 2 * H, 7, 9, nc.sync)
        load_packed(2, nc.sync)
        for r in (0, 1):
            load_scale_row(s2[:], s2_rows, 0, r, nc.sync)
        load_weights(wp, "wp", wp_src, 4 * H, 7, 9, nc.sync)
        load_weights(w2, "w2", w2_src, 2 * N, 0, 4, nc.sync)
        load_weights(w1, "w1", w1_src, 2 * H, 9, 11, nc.sync)
        load_weights(wp, "wp", wp_src, 4 * H, 9, 11, nc.sync)
        load_weights(w1, "w1", w1_src, 2 * H, 11, 12, nc.sync)
        load_weights(wp, "wp", wp_src, 4 * H, 11, 12, nc.sync)
        load_weights(w2, "w2", w2_src, 2 * N, 4, 8, nc.sync)
        load_weights(w2, "w2", w2_src, 2 * N, 8, 12, nc.sync)

        x_window = xw[:].bitcast(U32)
        out_view = out.rearrange("(h p) s -> p h s", p=P)
        staged = keep.tile([P, 2, E * C], F32, name="staged")
        grouped = {}
        first_four = shared.tile([P, 4 * 4 * C], BF16, name="first_four", align_bytes=64, offset=HELD_AT[1])
        activated = {}

        windows = (x_window, xs[:])
        lists = (own_list, partner_list)
        picked = {}

        def gather(batch):
            at = HELD_AT[batch - 1] if batch else None
            for side, sort, lo, hi in GATHERS[batch]:
                n = (hi - lo) * C
                dtype, size = ((U32, 4), (U8, 1))[sort]
                name = "picked_%d_%d_%d" % (side, sort, lo)
                if batch:
                    t = shared.tile([P, n], dtype, name=name, align_bytes=64, offset=at)
                    at = at + n * size
                else:
                    t = keep.tile([P, n], dtype, name=name, align_bytes=64)
                nc.vector.tensor_copy(t[:], windows[sort].indirect(lists[side][:, lo * C // 16 : hi * C // 16]))
                for e in range(lo, hi):
                    picked[side, sort, e] = t[:, (e - lo) * C : (e - lo + 1) * C]

        def first_layer(i):
            lo, hi = FIRST[i]
            for e in range(lo, hi):
                plane, at = (early, e) if e < EARLY else (late, e - EARLY)
                pre = psum.tile([P, H], F32, name="pre_%d" % e, offset=(e % 4) * BANK)
                moving = (
                    (w1[e].bitcast(FP4X4), plane[:, at, :]),
                    (wp[e].bitcast(FP8X4), packed[e // 4][4 * (e % 4) : P, :]),
                )
                sides = (1, 0) if e == 0 else (0, 1)
                for side in sides:
                    nc.tensor.matmul_mx(
                        out=pre[:], lhsT=picked[side, WORDS, e].bitcast(FP8X4), lhsT_scale=picked[side, BYTES, e],
                        rhs=moving[side][0], rhs_scale=moving[side][1], start=side == sides[0], stop=side == sides[1],
                    )
                h = keep.tile([P, H], BF16, name="h_%d" % e, align_bytes=64)
                nc.scalar.activation(
                    h[:].rearrange("s (u p d) -> s u p d", u=2, d=2),
                    pre[:].rearrange("s (p u d) -> s u p d", u=2, d=2),
                    SILU,
                    bias=warm_out[:],
                )
                activated[e] = h

        def turn(i):
            lo, hi = GROUPS[i]
            n = (hi - lo) * C
            turned = psum.tile([P, hi - lo, 2, C], F32, name="turned_%d" % lo, offset=TURN_BANK[i] * BANK)
            for e in range(lo, hi):
                pairs = activated[e][:].bitcast(F32)
                for u in range(2):
                    nc.tensor.transpose(turned[:, e - lo, u, :], pairs[:, u * P : (u + 1) * P], ident[:])
            if i < 2:
                ht = first_four[:, 4 * lo * C : 4 * hi * C]
            else:
                ht = keep.tile([P, 4 * n], BF16, name="ht_%d" % lo, align_bytes=64)
            copy = nc.vector.tensor_copy if i in TURN_ON_VECTOR else nc.scalar.copy
            copy(
                ht[:, 0 : 4 * n].bitcast(F32).rearrange("p (e s u) -> p e s u", u=2, s=C),
                turned[:].rearrange("p e u s -> p e s u"),
            )
            grouped[lo] = ht

        quantised = {}

        def quantise(i):
            lo, hi = GROUPS[i]
            n = (hi - lo) * C
            codes = keep.tile([P, n], U32, name="h_codes_%d" % lo, align_bytes=64)
            scales = keep.tile([P, n], U8, name="h_scales_%d" % lo, align_bytes=64)
            nc.vector.quantize_mx(out=codes[:].bitcast(FP8X4), scales=scales[:], in_=grouped[lo][:, 0 : 4 * n])
            quantised[i] = (codes, scales)

        def quantise_first_four():
            codes = keep.tile([P, 4 * C], U32, name="h_codes_first", align_bytes=64)
            scales = keep.tile([P, 4 * C], U8, name="h_scales_first", align_bytes=64)
            nc.vector.quantize_mx(out=codes[:].bitcast(FP8X4), scales=scales[:], in_=first_four[:])
            for i in range(2):
                quantised[i] = (codes[:, 2 * C * i : 2 * C * (i + 1)], scales[:, 2 * C * i : 2 * C * (i + 1)])

        def product(y, e, half, codes, scales):
            nc.tensor.matmul_mx(
                out=y,
                lhsT=w2[e][:, half * 2 * P : (half + 1) * 2 * P].bitcast(FP4X4),
                lhsT_scale=s2[:, e, half * P : (half + 1) * P],
                rhs=codes.bitcast(FP8X4), rhs_scale=scales, start=True, stop=True,
            )

        def store(hi):
            cols = slice(STORE_FROM[hi] * C, hi * C)
            nc.sync.dma_start(out=out_view[:, :, cols], in_=staged[:, :, cols])

        def second_layer(i):
            lo, hi = GROUPS[i]
            n = (hi - lo) * C
            codes, scales = quantised[i]
            y = psum.tile([P, 2, n], F32, name="y_%d" % lo, offset=Y_BANK[i] * BANK)
            for e in range(lo, hi):
                sl = slice((e - lo) * C, (e - lo + 1) * C)
                for half in range(2):
                    product(y[:, half, sl], e, half, codes[:, sl], scales[:, sl])
            copy = nc.vector.tensor_copy if i in Y_ON_VECTOR else nc.scalar.copy
            copy(staged[:, :, lo * C : hi * C], y[:])
            if hi in STORE_FROM:
                store(hi)

        def last_expert():
            codes, scales = quantised[len(GROUPS) - 1]
            for half, copy in enumerate((nc.scalar.copy, nc.vector.tensor_copy)):
                y = psum.tile([P, C], F32, name="y_last_%d" % half, offset=LAST_BANKS[half] * BANK)
                product(y[:], E - 1, half, codes[:], scales[:])
                copy(staged[:, half, (E - 1) * C : E * C], y[:])
            store(E)

        gather(0)
        gather(1)
        first_layer(0)
        first_layer(1)
        turn(0)
        first_layer(2)
        turn(1)
        first_layer(3)
        turn(2)
        quantise_first_four()
        gather(2)
        first_layer(4)
        turn(3)
        second_layer(0)
        second_layer(1)
        first_layer(5)
        first_layer(6)
        quantise(2)
        quantise(3)
        turn(4)
        quantise(4)
        second_layer(2)
        turn(5)
        turn(6)
        second_layer(3)
        turn(7)
        second_layer(4)
        for i in range(5, 8):
            quantise(i)
        for i in range(5, 7):
            second_layer(i)
        last_expert()
